import numpy as np
import ml_dtypes


def mxq(x, axis, fmt="e4m3"):
    dtype, down = {"e4m3": (ml_dtypes.float8_e4m3fn, 7), "e5m2": (ml_dtypes.float8_e5m2, 14)}[fmt]
    v = np.moveaxis(np.asarray(x, np.float32).astype(ml_dtypes.bfloat16).astype(np.float64), axis, -1)
    blocks = v.reshape(v.shape[:-1] + (-1, 32))
    amax = np.abs(blocks).max(-1, keepdims=True)
    byte = np.maximum(np.where(amax > 0, np.frexp(amax)[1] - 1 + 127, 0) - down, 1)
    scale = np.exp2(byte - 127.0)
    codes = (blocks / scale).astype(np.float32).astype(dtype).astype(np.float64)
    return np.moveaxis((codes * scale).reshape(v.shape), -1, axis)


WIDE = False


def mx_kscale(k):
    if not WIDE:
        return np.ones(k)
    levels = np.array([10, -10, 5, -5, 0])
    if k % 512:
        return np.exp2(np.random.permutation(np.resize(levels, k // 32))).repeat(32)
    a = np.empty((k // 512, 16))
    for p in range(k // 512):
        a[p, :8] = np.random.permutation(np.resize(levels, 8))
        for g in range(8):
            far = levels[np.abs(levels - a[p, g]) >= 10]
            a[p, g + 8] = far[np.random.randint(len(far))]
    return np.exp2(a.ravel()).repeat(32)


def f64(x):
    return np.asarray(x).astype(np.float64)


def striped(idx):
    return np.tile(idx.reshape(-1, 16).T, (8, 1)).astype(np.uint16)


def unstriped(offs):
    return offs[:16].T.reshape(-1).astype(np.int64)


def pack_weight(w):
    k, n = w.shape
    w = f64(np.asarray(w, np.float32).astype(ml_dtypes.bfloat16)).reshape(k // 32, 32, n)
    amax = np.abs(w).max(1)
    byte = np.clip(np.where(amax > 0, np.frexp(amax)[1] - 1 + 127 - 7, 1), 1, 254)
    scaled = (w * np.exp2(127.0 - byte)[:, None, :]).reshape(k, n).astype(np.float32)
    words = np.ascontiguousarray(scaled.reshape(k // 512, 128, 4, n).transpose(0, 1, 3, 2)).astype(ml_dtypes.float8_e4m3fn).view(np.uint8)
    return words, np.ascontiguousarray(byte.astype(np.uint8).reshape(k // 512, 16, n))


def unpack_weight(words, scales):
    g, p, n, _ = words.shape
    vals = np.ascontiguousarray(words).view(ml_dtypes.float8_e4m3fn).astype(np.float64) * np.repeat(np.exp2(scales.astype(np.float64) - 127.0), 8, axis=1)[..., None]
    return vals.transpose(0, 1, 3, 2).reshape(g * 512, n)


E2M1 = np.array([0.0, 0.5, 1.0, 1.5, 2.0, 3.0, 4.0, 6.0, -0.0, -0.5, -1.0, -1.5, -2.0, -3.0, -4.0, -6.0])


def pack_fp4(w):
    k, n = w.shape
    w = f64(np.asarray(w, np.float32).astype(ml_dtypes.bfloat16)).reshape(k // 32, 32, n)
    amax = np.abs(w).max(1)
    mant, ex = np.frexp(amax / 6.0)
    byte = np.clip(np.where(amax > 0, np.where(mant > 0.5, ex, ex - 1) + 127, 1), 1, 254)
    scaled = (w * np.exp2(127.0 - byte)[:, None, :]).reshape(k, n).astype(np.float32)
    c = np.ascontiguousarray(scaled.reshape(k // 512, 128, 4, n).transpose(0, 1, 3, 2)).astype(ml_dtypes.float4_e2m1fn).view(np.uint8) & 0xF
    words = (c[..., 0::2] | (c[..., 1::2] << 4)).reshape(k // 512, 128, 2 * n)
    return np.ascontiguousarray(words), np.ascontiguousarray(byte.astype(np.uint8).reshape(k // 512, 16, n))


def unpack_fp4(words, scales):
    g, _, n = scales.shape
    words = np.ascontiguousarray(words).reshape(g, 128, n, 2)
    nib = np.empty((g, 128, n, 4), np.uint8)
    nib[..., 0::2] = words & 0xF
    nib[..., 1::2] = words >> 4
    vals = E2M1[nib] * np.repeat(np.exp2(scales.astype(np.float64) - 127.0), 8, axis=1)[..., None]
    return vals.transpose(0, 1, 3, 2).reshape(g * 512, n)


def planes(y):
    n, m = y.shape
    v = y.astype(np.float32).astype(ml_dtypes.bfloat16).astype(np.float64).reshape(n // 32, 32, m)
    top = np.abs(v).max(1)
    byte = np.clip(np.where(top > 0, np.frexp(top)[1] - 1 + 127 - 7, 1), 1, 254)
    codes = (v * np.exp2(127.0 - byte)[:, None, :]).reshape(n, m).astype(np.float32).astype(ml_dtypes.float8_e4m3fn).view(np.uint8)
    words = codes.reshape(n // 512, 128, 4, m).transpose(0, 1, 3, 2)
    return np.ascontiguousarray(words), np.ascontiguousarray(byte.astype(np.uint8).reshape(n // 512, 16, m))


K, T, S, H, Z, W = 512, 1024, 512, 512, 512, 1024
P = 2 ** 7


def setup_inputs():
    n = np.random.standard_normal
    s = mx_kscale(K)[:, None]
    u = mx_kscale(H)
    packed_xT = pack_weight(n((K, T)) * s)
    packed_w1 = pack_fp4(n((K, H)) / np.sqrt(K) / s)
    packed_w2 = pack_fp4(n((K, H)) / np.sqrt(K) / s)
    packed_eT = pack_weight(n((K, W)) * s)
    packed_w3 = pack_fp4(n((K, H)) / np.sqrt(K) / s)
    return {
        "x_words": packed_xT[0],
        "x_scales": packed_xT[1],
        "w1_words": packed_w1[0],
        "w1_scales": packed_w1[1],
        "w2_words": packed_w2[0],
        "w2_scales": packed_w2[1],
        "e_words": packed_eT[0],
        "e_scales": packed_eT[1],
        "w3_words": packed_w3[0],
        "w3_scales": packed_w3[1],
        "unit": (np.random.uniform(0.6, 1.4, (H, 1)) * u[:, None]).astype(np.float32),
        "unit2": (np.random.uniform(0.6, 1.4, (H, 1)) / np.sqrt(H) / u[:, None]).astype(np.float32),
        "noi": (np.tile(np.random.uniform(0.3, 1.0, W), (P, 1))).astype(np.float32),
        "offs": striped(np.random.permutation(T)[:S]),
        "txb": striped(np.random.permutation(W)[:Z]),
        "pol": striped(np.random.permutation(S)),
        "adj": striped(np.random.permutation(Z)),
    }


def reference(x_words, x_scales, w1_words, w1_scales, w2_words, w2_scales, e_words, e_scales, w3_words, w3_scales, unit, unit2, noi, offs, txb, pol, adj):
    xq = unpack_weight(x_words, x_scales)[:, unstriped(offs)]
    re = unpack_fp4(w1_words, w1_scales).T @ xq
    im2 = unpack_fp4(w2_words, w2_scales).T @ xq
    ip = im2[:, unstriped(pol)]
    rx = re * np.tanh(ip) + 0.4 * re
    hid = f64(unit) * rx
    e_txb = unpack_weight(e_words, e_scales)[:, unstriped(txb)]
    ye = unpack_fp4(w3_words, w3_scales).T @ e_txb
    hid2 = f64(unit2) * ye
    sc = mxq(hid, 0, "e4m3").T @ mxq(hid2, 0, "e4m3")
    pow_ = (sc) ** 2
    itf = 0.5 * pow_[:, unstriped(adj)]
    sinr = pow_ / (itf + f64(noi)[:1][:, unstriped(txb)] + 0.2)
    out_0 = (sinr / (sinr + 1.5)) * sc
    return (out_0,) + planes(out_0)

@@ -1,0 +1,270 @@
+from contextlib import ExitStack
+
+import concourse.mybir as mybir
+from concourse.masks import make_identity
+
+F32 = mybir.dt.float32
+BF16 = mybir.dt.bfloat16
+I32 = mybir.dt.int32
+U32 = mybir.dt.uint32
+U16 = mybir.dt.uint16
+U8 = mybir.dt.uint8
+FP8X4 = mybir.dt.float8_e4m3fn_x4
+FP4X4 = mybir.dt.float4_e2m1fn_x4
+ACT = mybir.ActivationFunctionType
+ALU = mybir.AluOpType
+
+P = 128
+S = 512
+STORE = 1024
+FLOPS = 4 * 2 * 512 * 512 * 512
+
+
+def tile_picked_ybeamsl_sat_po_kernel(
+    tc, x_words, x_scales, w1_words, w1_scales, w2_words, w2_scales, e_words, e_scales,
+    w3_words, w3_scales, unit, unit2, noi, offs, txb, pol, adj, out_0, out_1, out_2,
+):
+    nc = tc.nc
+    with ExitStack() as ctx:
+        sb = ctx.enter_context(tc.tile_pool(name="sb", bufs=1))
+        ps = ctx.enter_context(tc.psum_pool(name="ps", bufs=1))
+
+        def buf(shape, dtype, name):
+            return sb.tile(shape, dtype, name=name, align_bytes=64)
+
+        def bank(b, name):
+            return ps.tile([P, S], F32, name=name, tag="bank%d" % b)
+
+        def load_list(src, name):
+            t = sb.tile([P, S // 16], U16, name=name)
+            nc.sync.dma_start(t[:], src)
+            return t
+
+        def scale_tile(width, name):
+            t = buf([P, width], U8, name)
+            nc.vector.memset(t[:].bitcast(I32), 0)
+            return t
+
+        def load_scales(t, src, queue):
+            for q in range(4):
+                queue.dma_start(t[32 * q : 32 * q + 4, :].bitcast(I32), src[0, 4 * q : 4 * q + 4, :].bitcast(I32))
+
+        def load_words(src, name):
+            t = buf([P, STORE], U32, name)
+            nc.sync.dma_start(t[:].bitcast(I32), src[0].rearrange("p n t -> p (n t)").bitcast(I32))
+            return t
+
+        def load_fp4(src, name):
+            t = buf([P, 2 * S], U8, name)
+            nc.sync.dma_start(t[:].bitcast(I32), src[0].bitcast(I32))
+            return t
+
+        def deal(words, scales, name):
+            dw = buf([P, 2 * S], U8, name + "_dw")
+            ds = buf([P, S], U8, name + "_ds")
+            nc.vector.tensor_copy(
+                dw[:].bitcast(I32).rearrange("p (t b j) -> p t b j", t=4, j=4),
+                words[:].bitcast(I32).rearrange("p (b t j) -> p t b j", t=4, j=4),
+            )
+            nc.vector.tensor_copy(
+                ds[:].bitcast(I32).rearrange("p (t b j) -> p t b j", t=4, j=2),
+                scales[:].bitcast(I32).rearrange("p (b t j) -> p t b j", t=4, j=2),
+            )
+            return dw, ds
+
+        def weight_pass(out, w, t, codes, scales, cols):
+            nc.tensor.matmul_mx(
+                out=out,
+                lhsT=w[0][:, 256 * t : 256 * (t + 1)].bitcast(FP4X4),
+                lhsT_scale=w[1][:, P * t : P * (t + 1)],
+                rhs=codes[:, cols].bitcast(FP8X4),
+                rhs_scale=scales[:, cols],
+                start=True,
+                stop=True,
+            )
+
+        ident = buf([P, P], F32, "ident")
+        make_identity(nc, ident[:])
+        xs = scale_tile(STORE, "xs")
+        es = scale_tile(STORE, "es")
+        w2s = scale_tile(S, "w2s")
+        noise = buf([P, STORE], F32, "noise")
+        nc.vector.memset(noise[:], 0.0)
+        unit_rows = buf([P, P], F32, "unit_rows")
+        nc.vector.memset(unit_rows[:], 0.0)
+        w1s = scale_tile(S, "w1s")
+        w3s = scale_tile(S, "w3s")
+        leak = buf([P, 256], F32, "leak")
+        nc.vector.memset(leak[:], 0.75)
+
+        offs_t = load_list(offs, "offs_t")
+        load_scales(xs, x_scales, nc.sync)
+        xw = load_words(x_words, "xw")
+        txb_t = load_list(txb, "txb_t")
+        w2w = load_fp4(w2_words, "w2w")
+        load_scales(es, e_scales, nc.gpsimd)
+        load_scales(w2s, w2_scales, nc.sync)
+        nc.sync.dma_start(noise[0:1, :], noi[0:1, :])
+        ew = load_words(e_words, "ew")
+        for a, u in enumerate((unit, unit2)):
+            nc.sync.dma_start(
+                unit_rows[4 * a : 4 * a + 4, :].rearrange("t (b r) -> t b r", r=8),
+                u.rearrange("(b t r) o -> t b (r o)", t=4, r=8),
+            )
+        w3w = load_fp4(w3_words, "w3w")
+        load_scales(w3s, w3_scales, nc.sync)
+        pol_t = load_list(pol, "pol_t")
+        w1w = load_fp4(w1_words, "w1w")
+        load_scales(w1s, w1_scales, nc.gpsimd)
+        adj_t = load_list(adj, "adj_t")
+
+        xq_s = buf([P, S], U8, "xq_s")
+        nc.vector.tensor_copy(xq_s[:], xs[:].indirect(offs_t[:]))
+        xq = buf([P, S], U32, "xq")
+        nc.vector.tensor_copy(xq[:], xw[:].indirect(offs_t[:]))
+        w2 = deal(w2w, w2s, "w2")
+
+        unit_ps = bank(7, "unit_ps")
+        nc.tensor.transpose(unit_ps[:, 0:P], unit_rows[:], ident[:])
+        units = buf([P, 8], F32, "units")
+        nc.scalar.copy(units[:], unit_ps[:, 0:8])
+
+        noise_rows = buf([P, S], F32, "noise_rows")
+        nc.scalar.activation(noise_rows[:], noise[:].indirect(txb_t[:]), ACT.Copy, bias=0.3, scale=1.5)
+        noise_ps = bank(6, "noise_ps")
+        for c in range(4):
+            nc.tensor.transpose(noise_ps[:, P * c : P * (c + 1)], noise_rows[:, P * c : P * (c + 1)], ident[:])
+        floor = buf([P, 4], F32, "floor")
+        nc.scalar.copy(floor[:], noise_ps[:, 0:S:P])
+
+        gate = []
+        th = []
+        for t in range(4):
+            im = bank(t, "im%d" % t)
+            weight_pass(im[:], w2, t, xq, xq_s, slice(0, S))
+            th.append(buf([P, S], F32, "th%d" % t))
+            nc.scalar.activation(th[t][:], im[:], ACT.Tanh)
+
+        eq = buf([P, S], U32, "eq")
+        nc.vector.tensor_copy(eq[:], ew[:].indirect(txb_t[:]))
+        eq_s = buf([P, S], U8, "eq_s")
+        for t in range(4):
+            gate.append(buf([P, S], F32, "gate%d" % t))
+            nc.vector.tensor_scalar(gate[t][:], th[t][:], 0.4, units[:, t : t + 1], ALU.add, ALU.mult)
+            if t == 1:
+                nc.vector.tensor_copy(eq_s[:], es[:].indirect(txb_t[:]))
+        w3 = deal(w3w, w3s, "w3")
+        w1 = deal(w1w, w1s, "w1")
+
+        hid2 = buf([P, S, 4], BF16, "hid2")
+        hid = buf([P, 4, P, 4], BF16, "hid")
+        ye = []
+        re = []
+        for c in range(4):
+            ye.append(bank(4 + c, "ye%d" % c))
+            for t in range(4):
+                weight_pass(ye[c][:, P * t : P * (t + 1)], w3, t, eq, eq_s, slice(P * c, P * (c + 1)))
+        for c in range(4):
+            re.append(bank(c, "re%d" % c))
+            for t in range(4):
+                weight_pass(re[c][:, P * t : P * (t + 1)], w1, t, xq, xq_s, slice(P * c, P * (c + 1)))
+        picked = []
+        for c in range(4):
+            picked.append(buf([P, 4, P], F32, "picked%d" % c))
+            for t in range(4):
+                nc.scalar.activation(picked[c][:, t, :], gate[t][:].indirect(pol_t[:, 8 * c : 8 * (c + 1)]), ACT.Copy)
+        for c in range(4):
+            nc.vector.tensor_tensor(
+                hid2[:, P * c : P * (c + 1), :],
+                ye[c][:].rearrange("p (t n) -> p n t", t=4),
+                units[:, 4:8].unsqueeze(1).to_broadcast([P, P, 4]),
+                ALU.mult,
+            )
+        h2q = buf([P, S], U32, "h2q")
+        h2s = buf([P, S], U8, "h2s")
+        for c in range(4):
+            nc.vector.tensor_tensor(
+                hid[:, :, 32 * c : 32 * (c + 1), :].rearrange("p r m t -> p m t r"),
+                re[c][:].rearrange("p (t m r) -> p m t r", t=4, r=4),
+                picked[c][:].rearrange("p t (m r) -> p m t r", r=4),
+                ALU.mult,
+            )
+            if c == 0:
+                nc.vector.quantize_mx(out=h2q[:].bitcast(FP8X4), scales=h2s[:], in_=hid2[:].rearrange("p n t -> p (n t)"))
+
+        sc = []
+        power = []
+        for r in range(4):
+            hq = buf([P, P], U32, "hq%d" % r)
+            hs = buf([P, P], U8, "hs%d" % r)
+            nc.vector.quantize_mx(out=hq[:].bitcast(FP8X4), scales=hs[:], in_=hid[:, r].rearrange("p m t -> p (m t)"))
+            sc.append(bank(4 + r, "sc%d" % r))
+            nc.tensor.matmul_mx(
+                out=sc[r][:], lhsT=hq[:].bitcast(FP8X4), lhsT_scale=hs[:],
+                rhs=h2q[:].bitcast(FP8X4), rhs_scale=h2s[:], start=True, stop=True,
+            )
+            power.append(buf([P, S], F32, "power%d" % r))
+            nc.scalar.activation(power[r][:], sc[r][:], ACT.Square)
+
+        H = 256
+        out_rows = out_0.rearrange("(p r) e -> p r e", r=4)
+        oq = buf([P, S], U32, "oq")
+        osc = buf([P, S], U8, "osc")
+        result = [buf([P, 4, H], F32, "result%d" % h) for h in range(2)]
+        units_order = [(h, r) for h in range(2) for r in range(4)]
+        work = {}
+
+        def front(h, r):
+            leaked = buf([P, H], F32, "leaked%d%d" % (h, r))
+            window = power[r][:].indirect(adj_t[:, 16 * h : 16 * (h + 1)])
+            if h == 0:
+                nc.vector.tensor_tensor(leaked[:], window, leak[:], ALU.mult)
+            else:
+                nc.scalar.activation(leaked[:], window, ACT.Copy, scale=0.75)
+            acc = bank(r, "acc%d%d" % (h, r))
+            for b in range(2):
+                cols = slice(P * b, P * (b + 1))
+                nc.tensor.matmul(acc[:, cols], power[r][:, H * h + P * b : H * h + P * (b + 1)], ident[:],
+                                 start=True, stop=False, is_transpose=True)
+                nc.tensor.matmul(acc[:, cols], leaked[:, cols], ident[:], start=False, stop=True, is_transpose=True)
+            work[(h, r)] = acc
+
+        def middle(h, r):
+            acc = work[(h, r)]
+            root = buf([P, H], F32, "root%d%d" % (h, r))
+            for b in range(2):
+                cols = slice(P * b, P * (b + 1))
+                nc.scalar.activation(root[:, cols], acc[:, cols], ACT.Abs_reciprocal_sqrt,
+                                     bias=floor[:, 2 * h + b : 2 * h + b + 1])
+            inv = buf([P, H], F32, "inv%d%d" % (h, r))
+            nc.scalar.activation(inv[:], root[:], ACT.Square)
+            for b in range(2):
+                nc.tensor.transpose(acc[:, H + P * b : H + P * (b + 1)], inv[:, P * b : P * (b + 1)], ident[:])
+
+        def back(h, r):
+            acc = work[(h, r)]
+            cols = slice(H * h, H * (h + 1))
+            share = buf([P, H], F32, "share%d%d" % (h, r))
+            nc.vector.tensor_tensor(share[:], acc[:, H:S], power[r][:, cols], ALU.mult)
+            nc.vector.tensor_tensor(result[h][:, r, :], sc[r][:, cols], share[:], ALU.mult)
+            nc.sync.dma_start(out_rows[:, r, cols], result[h][:, r, :])
+            if r == 3:
+                rounded = buf([P, H, 4], BF16, "rounded%d" % h)
+                nc.vector.tensor_copy(rounded[:], result[h][:].rearrange("p r e -> p e r"))
+                nc.vector.quantize_mx(out=oq[:, cols].bitcast(FP8X4), scales=osc[:, cols],
+                                      in_=rounded[:].rearrange("p e r -> p (e r)"))
+                nc.sync.dma_start(
+                    out_1[0].rearrange("p n t -> p (n t)").bitcast(I32)[:, cols], oq[:, cols].bitcast(I32)
+                )
+
+        n = len(units_order)
+        for step in range(n + 3):
+            if step < n:
+                front(*units_order[step])
+            if 0 <= step - 1 < n:
+                middle(*units_order[step - 1])
+            if 0 <= step - 3 < n:
+                back(*units_order[step - 3])
+        for q in range(4):
+            queue = nc.sync if q % 2 == 0 else nc.scalar
+            queue.dma_start(out_2[0, 4 * q : 4 * q + 4, :].bitcast(I32), osc[32 * q : 32 * q + 4, :].bitcast(I32))

@@ -17,6 +17,7 @@ ALU = mybir.AluOpType
 P = 128
 S = 512
 STORE = 1024
+H = 256
 FLOPS = 4 * 2 * 512 * 512 * 512
 
 
@@ -29,8 +30,8 @@ def tile_picked_ybeamsl_sat_po_kernel(
         sb = ctx.enter_context(tc.tile_pool(name="sb", bufs=1))
         ps = ctx.enter_context(tc.psum_pool(name="ps", bufs=1))
 
-        def buf(shape, dtype, name):
-            return sb.tile(shape, dtype, name=name, align_bytes=64)
+        def buf(shape, dtype, name, tag=""):
+            return sb.tile(shape, dtype, name=name, tag=tag or name, align_bytes=64)
 
         def bank(b, name):
             return ps.tile([P, S], F32, name=name, tag="bank%d" % b)
@@ -40,13 +41,13 @@ def tile_picked_ybeamsl_sat_po_kernel(
             nc.sync.dma_start(t[:], src)
             return t
 
-        def scale_tile(width, name):
+        def scale_tile(width, name, engine):
             t = buf([P, width], U8, name)
-            nc.vector.memset(t[:].bitcast(I32), 0)
+            engine.memset(t[:].bitcast(I32), 0)
             return t
 
-        def load_scales(t, src, queue):
-            for q in range(4):
+        def load_scales(t, src, queues, first=0):
+            for q, queue in enumerate(queues, first):
                 queue.dma_start(t[32 * q : 32 * q + 4, :].bitcast(I32), src[0, 4 * q : 4 * q + 4, :].bitcast(I32))
 
         def load_words(src, name):
@@ -59,14 +60,14 @@ def tile_picked_ybeamsl_sat_po_kernel(
             nc.sync.dma_start(t[:].bitcast(I32), src[0].bitcast(I32))
             return t
 
-        def deal(words, scales, name):
+        def deal(words, scales, name, engine):
             dw = buf([P, 2 * S], U8, name + "_dw")
             ds = buf([P, S], U8, name + "_ds")
-            nc.vector.tensor_copy(
+            engine.tensor_copy(
                 dw[:].bitcast(I32).rearrange("p (t b j) -> p t b j", t=4, j=4),
                 words[:].bitcast(I32).rearrange("p (b t j) -> p t b j", t=4, j=4),
             )
-            nc.vector.tensor_copy(
+            engine.tensor_copy(
                 ds[:].bitcast(I32).rearrange("p (t b j) -> p t b j", t=4, j=2),
                 scales[:].bitcast(I32).rearrange("p (b t j) -> p t b j", t=4, j=2),
             )
@@ -83,78 +84,73 @@ def tile_picked_ybeamsl_sat_po_kernel(
                 stop=True,
             )
 
-        ident = buf([P, P], F32, "ident")
-        make_identity(nc, ident[:])
-        xs = scale_tile(STORE, "xs")
-        es = scale_tile(STORE, "es")
-        w2s = scale_tile(S, "w2s")
-        noise = buf([P, STORE], F32, "noise")
-        nc.vector.memset(noise[:], 0.0)
+        xs = scale_tile(STORE, "xs", nc.gpsimd)
+        w2s = scale_tile(S, "w2s", nc.gpsimd)
+        load_scales(w2s, w2_scales, [nc.gpsimd], 3)
         unit_rows = buf([P, P], F32, "unit_rows")
         nc.vector.memset(unit_rows[:], 0.0)
-        w1s = scale_tile(S, "w1s")
-        w3s = scale_tile(S, "w3s")
-        leak = buf([P, 256], F32, "leak")
-        nc.vector.memset(leak[:], 0.75)
-
-        offs_t = load_list(offs, "offs_t")
-        load_scales(xs, x_scales, nc.sync)
-        xw = load_words(x_words, "xw")
-        txb_t = load_list(txb, "txb_t")
-        w2w = load_fp4(w2_words, "w2w")
-        load_scales(es, e_scales, nc.gpsimd)
-        load_scales(w2s, w2_scales, nc.sync)
-        nc.sync.dma_start(noise[0:1, :], noi[0:1, :])
-        ew = load_words(e_words, "ew")
         for a, u in enumerate((unit, unit2)):
-            nc.sync.dma_start(
+            nc.gpsimd.dma_start(
                 unit_rows[4 * a : 4 * a + 4, :].rearrange("t (b r) -> t b r", r=8),
                 u.rearrange("(b t r) o -> t b (r o)", t=4, r=8),
             )
+        ident = buf([P, P], F32, "ident")
+        make_identity(nc, ident[:])
+        noise = buf([P, STORE], F32, "noise")
+        nc.vector.memset(noise[:], 0.0)
+        es = scale_tile(STORE, "es", nc.vector)
+        w3s = scale_tile(S, "w3s", nc.vector)
+        w1s = scale_tile(S, "w1s", nc.vector)
+        leak = buf([P, H], F32, "leak")
+        nc.vector.memset(leak[:], 0.75)
+
+        load_scales(xs, x_scales, (nc.scalar, nc.scalar), 0)
+        offs_t = load_list(offs, "offs_t")
+        load_scales(xs, x_scales, (nc.sync, nc.sync), 2)
+        xw = load_words(x_words, "xw")
+        txb_t = load_list(txb, "txb_t")
+        w2w = load_fp4(w2_words, "w2w")
+        nc.sync.dma_start(noise[0:1, :], noi[0:1, :])
+        load_scales(w2s, w2_scales, [nc.sync] * 3)
+        ew = load_words(e_words, "ew")
+        load_scales(es, e_scales, [nc.sync] * 4)
         w3w = load_fp4(w3_words, "w3w")
-        load_scales(w3s, w3_scales, nc.sync)
+        load_scales(w3s, w3_scales, [nc.sync] * 4)
         pol_t = load_list(pol, "pol_t")
         w1w = load_fp4(w1_words, "w1w")
-        load_scales(w1s, w1_scales, nc.gpsimd)
+        load_scales(w1s, w1_scales, [nc.sync] * 4)
         adj_t = load_list(adj, "adj_t")
 
         xq_s = buf([P, S], U8, "xq_s")
         nc.vector.tensor_copy(xq_s[:], xs[:].indirect(offs_t[:]))
         xq = buf([P, S], U32, "xq")
         nc.vector.tensor_copy(xq[:], xw[:].indirect(offs_t[:]))
-        w2 = deal(w2w, w2s, "w2")
-
-        unit_ps = bank(7, "unit_ps")
-        nc.tensor.transpose(unit_ps[:, 0:P], unit_rows[:], ident[:])
-        units = buf([P, 8], F32, "units")
-        nc.scalar.copy(units[:], unit_ps[:, 0:8])
+        w2 = deal(w2w, w2s, "w2", nc.vector)
 
         noise_rows = buf([P, S], F32, "noise_rows")
         nc.scalar.activation(noise_rows[:], noise[:].indirect(txb_t[:]), ACT.Copy, bias=0.3, scale=1.5)
-        noise_ps = bank(6, "noise_ps")
-        for c in range(4):
-            nc.tensor.transpose(noise_ps[:, P * c : P * (c + 1)], noise_rows[:, P * c : P * (c + 1)], ident[:])
-        floor = buf([P, 4], F32, "floor")
-        nc.scalar.copy(floor[:], noise_ps[:, 0:S:P])
 
         gate = []
         th = []
         for t in range(4):
             im = bank(t, "im%d" % t)
             weight_pass(im[:], w2, t, xq, xq_s, slice(0, S))
-            th.append(buf([P, S], F32, "th%d" % t))
+            th.append(buf([P, S], F32, "th%d" % t, ""))
             nc.scalar.activation(th[t][:], im[:], ACT.Tanh)
 
         eq = buf([P, S], U32, "eq")
         nc.vector.tensor_copy(eq[:], ew[:].indirect(txb_t[:]))
         eq_s = buf([P, S], U8, "eq_s")
+        nc.vector.tensor_copy(eq_s[:], es[:].indirect(txb_t[:]))
+        unit_ps = bank(0, "unit_ps")
+        nc.tensor.transpose(unit_ps[:, 0:P], unit_rows[:], ident[:])
+        units = buf([P, 8], F32, "units", "es")
+        nc.vector.tensor_copy(units[:], unit_ps[:, 0:8])
         for t in range(4):
             gate.append(buf([P, S], F32, "gate%d" % t))
             nc.vector.tensor_scalar(gate[t][:], th[t][:], 0.4, units[:, t : t + 1], ALU.add, ALU.mult)
-            if t == 1:
-                nc.vector.tensor_copy(eq_s[:], es[:].indirect(txb_t[:]))
-        w3 = deal(w3w, w3s, "w3")
-        w1 = deal(w1w, w1s, "w1")
+        w3 = deal(w3w, w3s, "w3", nc.gpsimd)
+        w1 = deal(w1w, w1s, "w1", nc.gpsimd)
 
         hid2 = buf([P, S, 4], BF16, "hid2")
         hid = buf([P, 4, P, 4], BF16, "hid")
@@ -172,7 +168,10 @@ def tile_picked_ybeamsl_sat_po_kernel(
         for c in range(4):
             picked.append(buf([P, 4, P], F32, "picked%d" % c))
             for t in range(4):
-                nc.scalar.activation(picked[c][:, t, :], gate[t][:].indirect(pol_t[:, 8 * c : 8 * (c + 1)]), ACT.Copy)
+                window = gate[t][:].indirect(pol_t[:, 8 * c : 8 * (c + 1)])
+                nc.scalar.activation(picked[c][:, t, :], window, ACT.Copy)
+        warm = buf([P, 1], F32, "warm")
+        nc.scalar.activation(warm[:], picked[3][:, 3, P - 1 : P], ACT.Abs_reciprocal_sqrt, bias=units[:, 0:1])
         for c in range(4):
             nc.vector.tensor_tensor(
                 hid2[:, P * c : P * (c + 1), :],
@@ -180,6 +179,11 @@ def tile_picked_ybeamsl_sat_po_kernel(
                 units[:, 4:8].unsqueeze(1).to_broadcast([P, P, 4]),
                 ALU.mult,
             )
+        noise_ps = bank(4, "noise_ps")
+        for c in range(4):
+            nc.tensor.transpose(noise_ps[:, P * c : P * (c + 1)], noise_rows[:, P * c : P * (c + 1)], ident[:])
+        floor = buf([P, 4], F32, "floor")
+        nc.vector.tensor_copy(floor[:], noise_ps[:, 0:S:P])
         h2q = buf([P, S], U32, "h2q")
         h2s = buf([P, S], U8, "h2s")
         for c in range(4):
@@ -206,65 +210,89 @@ def tile_picked_ybeamsl_sat_po_kernel(
             power.append(buf([P, S], F32, "power%d" % r))
             nc.scalar.activation(power[r][:], sc[r][:], ACT.Square)
 
-        H = 256
         out_rows = out_0.rearrange("(p r) e -> p r e", r=4)
         oq = buf([P, S], U32, "oq")
         osc = buf([P, S], U8, "osc")
         result = [buf([P, 4, H], F32, "result%d" % h) for h in range(2)]
-        units_order = [(h, r) for h in range(2) for r in range(4)]
-        work = {}
+        groups = [[(0,0)],[(1,0)],[(0,1),(1,1)],[(0,2),(0,3)],[(1,2),(1,3)]]
+        accs = {}
 
-        def front(h, r):
-            leaked = buf([P, H], F32, "leaked%d%d" % (h, r))
-            window = power[r][:].indirect(adj_t[:, 16 * h : 16 * (h + 1)])
-            if h == 0:
-                nc.vector.tensor_tensor(leaked[:], window, leak[:], ALU.mult)
-            else:
-                nc.scalar.activation(leaked[:], window, ACT.Copy, scale=0.75)
-            acc = bank(r, "acc%d%d" % (h, r))
-            for b in range(2):
-                cols = slice(P * b, P * (b + 1))
-                nc.tensor.matmul(acc[:, cols], power[r][:, H * h + P * b : H * h + P * (b + 1)], ident[:],
-                                 start=True, stop=False, is_transpose=True)
-                nc.tensor.matmul(acc[:, cols], leaked[:, cols], ident[:], start=False, stop=True, is_transpose=True)
-            work[(h, r)] = acc
+        def front(g):
+            acc = bank(g % 2, "acc%d" % g)
+            accs[g] = acc
+            for k, (h, r) in enumerate(groups[g]):
+                leaked = buf([P, H], F32, "leaked%d%d" % (h, r), "")
+                window = power[r][:].indirect(adj_t[:, 16 * h : 16 * (h + 1)])
+                if True:
+                    nc.vector.tensor_tensor(leaked[:], window, leak[:], ALU.mult)
+                else:
+                    nc.scalar.activation(leaked[:], window, ACT.Copy, scale=0.75)
+                for b in range(0, H, P):
+                    cols = slice(H * k + b, H * k + b + P)
+                    nc.tensor.matmul(acc[:, cols], power[r][:, H * h + b : H * h + b + P], ident[:],
+                                     start=True, stop=False, is_transpose=True)
+                    nc.tensor.matmul(acc[:, cols], leaked[:, b : b + P], ident[:], start=False, stop=True, is_transpose=True)
 
-        def middle(h, r):
-            acc = work[(h, r)]
-            root = buf([P, H], F32, "root%d%d" % (h, r))
-            for b in range(2):
-                cols = slice(P * b, P * (b + 1))
-                nc.scalar.activation(root[:, cols], acc[:, cols], ACT.Abs_reciprocal_sqrt,
-                                     bias=floor[:, 2 * h + b : 2 * h + b + 1])
-            inv = buf([P, H], F32, "inv%d%d" % (h, r))
+        def middle(g):
+            acc = accs[g]
+            width = H * len(groups[g])
+            root = buf([P, width], F32, "root%d" % g, "")
+            for j in sorted(set(2 * h + b for h, r in groups[g] for b in range(2))):
+                ks = [k for k, (h, r) in enumerate(groups[g]) if h == j // 2]
+                nc.scalar.activation(root[:].rearrange("p (k b n) -> p k b n", b=2, n=P)[:, ks[0] : ks[-1] + 1, j % 2, :],
+                                     acc[:, 0:width].rearrange("p (k b n) -> p k b n", b=2, n=P)[:, ks[0] : ks[-1] + 1, j % 2, :],
+                                     ACT.Abs_reciprocal_sqrt, bias=floor[:, j : j + 1])
+            inv = buf([P, width], F32, "inv%d" % g)
             nc.scalar.activation(inv[:], root[:], ACT.Square)
-            for b in range(2):
-                nc.tensor.transpose(acc[:, H + P * b : H + P * (b + 1)], inv[:, P * b : P * (b + 1)], ident[:])
+            if True:
+                acc = bank(2 + g % 2, "back%d" % g)
+                accs[g] = acc
+            for b in range(0, width, P):
+                nc.tensor.transpose(acc[:, b : b + P], inv[:, b : b + P], ident[:])
 
-        def back(h, r):
-            acc = work[(h, r)]
+        def back(g):
+            shares = []
+            for k, (h, r) in enumerate(groups[g]):
+                shares.append(buf([P, H], F32, "share%d%d" % (h, r)))
+                nc.vector.tensor_tensor(shares[k][:], accs[g][:, H * k : H * (k + 1)], power[r][:, H * h : H * (h + 1)], ALU.mult)
+            for k, (h, r) in enumerate(groups[g]):
+                cols = slice(H * h, H * (h + 1))
+                nc.vector.tensor_tensor(result[h][:, r, :], sc[r][:, cols], shares[k][:], ALU.mult)
+                nc.sync.dma_start(out_rows[:, r, cols], result[h][:, r, :])
+                if r == 3 and h == 0:
+                    round_cols(nc.scalar.copy, 0, 0, H)
+
+        rounded = {}
+
+        def round_cols(copy, h, c0, c1):
+            rounded[(h, c0)] = buf([P, c1 - c0, 4], BF16, "rounded%d_%d" % (h, c0))
+            copy(rounded[(h, c0)][:].rearrange("p (c i) r -> p c r i", i=4),
+                 result[h][:, :, c0:c1].rearrange("p r (c i) -> p c r i", i=4))
+
+        def emit(h, c0, c1):
+            cols = slice(H * h + c0, H * h + c1)
+            nc.vector.quantize_mx(out=oq[:, cols].bitcast(FP8X4), scales=osc[:, cols],
+                                  in_=rounded[(h, c0)][:].rearrange("p e r -> p (e r)"))
+
+        def store_words(h):
             cols = slice(H * h, H * (h + 1))
-            share = buf([P, H], F32, "share%d%d" % (h, r))
-            nc.vector.tensor_tensor(share[:], acc[:, H:S], power[r][:, cols], ALU.mult)
-            nc.vector.tensor_tensor(result[h][:, r, :], sc[r][:, cols], share[:], ALU.mult)
-            nc.sync.dma_start(out_rows[:, r, cols], result[h][:, r, :])
-            if r == 3:
-                rounded = buf([P, H, 4], BF16, "rounded%d" % h)
-                nc.vector.tensor_copy(rounded[:], result[h][:].rearrange("p r e -> p e r"))
-                nc.vector.quantize_mx(out=oq[:, cols].bitcast(FP8X4), scales=osc[:, cols],
-                                      in_=rounded[:].rearrange("p e r -> p (e r)"))
-                nc.sync.dma_start(
-                    out_1[0].rearrange("p n t -> p (n t)").bitcast(I32)[:, cols], oq[:, cols].bitcast(I32)
-                )
+            nc.sync.dma_start(out_1[0].rearrange("p n t -> p (n t)").bitcast(I32)[:, cols], oq[:, cols].bitcast(I32))
 
-        n = len(units_order)
+        n = len(groups)
         for step in range(n + 3):
             if step < n:
-                front(*units_order[step])
+                front(step)
             if 0 <= step - 1 < n:
-                middle(*units_order[step - 1])
-            if 0 <= step - 3 < n:
-                back(*units_order[step - 3])
+                middle(step - 1)
+            if 0 <= step - 2 < n:
+                back(step - 2)
+        round_cols(nc.vector.tensor_copy, 1, 0, P)
+        round_cols(nc.scalar.copy, 1, P, H)
+        emit(0, 0, H)
+        store_words(0)
+        emit(1, 0, P)
+        emit(1, P, H)
+        store_words(1)
         for q in range(4):
             queue = nc.sync if q % 2 == 0 else nc.scalar
             queue.dma_start(out_2[0, 4 * q : 4 * q + 4, :].bitcast(I32), osc[32 * q : 32 * q + 4, :].bitcast(I32))

@@ -88,7 +88,7 @@ def tile_picked_ybeamsl_sat_po_kernel(
         w2s = scale_tile(S, "w2s", nc.gpsimd)
         load_scales(w2s, w2_scales, [nc.gpsimd], 3)
         unit_rows = buf([P, P], F32, "unit_rows")
-        nc.vector.memset(unit_rows[:], 0.0)
+        nc.gpsimd.memset(unit_rows[:], 0.0)
         for a, u in enumerate((unit, unit2)):
             nc.gpsimd.dma_start(
                 unit_rows[4 * a : 4 * a + 4, :].rearrange("t (b r) -> t b r", r=8),
@@ -96,17 +96,18 @@ def tile_picked_ybeamsl_sat_po_kernel(
             )
         ident = buf([P, P], F32, "ident")
         make_identity(nc, ident[:])
+        leak = buf([P, H], F32, "leak")
+        nc.vector.memset(leak[:], 0.75)
         noise = buf([P, STORE], F32, "noise")
         nc.vector.memset(noise[:], 0.0)
         es = scale_tile(STORE, "es", nc.vector)
         w3s = scale_tile(S, "w3s", nc.vector)
         w1s = scale_tile(S, "w1s", nc.vector)
-        leak = buf([P, H], F32, "leak")
-        nc.vector.memset(leak[:], 0.75)
 
-        load_scales(xs, x_scales, (nc.scalar, nc.scalar), 0)
+        load_scales(xs, x_scales, (nc.scalar, nc.sync, nc.sync, nc.sync))
+        warm_tanh = buf([P, 1], F32, "warm_tanh")
+        nc.scalar.activation(warm_tanh[:], leak[:, 0:1], ACT.Tanh)
         offs_t = load_list(offs, "offs_t")
-        load_scales(xs, x_scales, (nc.sync, nc.sync), 2)
         xw = load_words(x_words, "xw")
         txb_t = load_list(txb, "txb_t")
         w2w = load_fp4(w2_words, "w2w")
@@ -130,7 +131,6 @@ def tile_picked_ybeamsl_sat_po_kernel(
         noise_rows = buf([P, S], F32, "noise_rows")
         nc.scalar.activation(noise_rows[:], noise[:].indirect(txb_t[:]), ACT.Copy, bias=0.3, scale=1.5)
 
-        gate = []
         th = []
         for t in range(4):
             im = bank(t, "im%d" % t)
@@ -146,32 +146,27 @@ def tile_picked_ybeamsl_sat_po_kernel(
         nc.tensor.transpose(unit_ps[:, 0:P], unit_rows[:], ident[:])
         units = buf([P, 8], F32, "units", "es")
         nc.vector.tensor_copy(units[:], unit_ps[:, 0:8])
-        for t in range(4):
-            gate.append(buf([P, S], F32, "gate%d" % t))
-            nc.vector.tensor_scalar(gate[t][:], th[t][:], 0.4, units[:, t : t + 1], ALU.add, ALU.mult)
         w3 = deal(w3w, w3s, "w3", nc.gpsimd)
         w1 = deal(w1w, w1s, "w1", nc.gpsimd)
 
         hid2 = buf([P, S, 4], BF16, "hid2")
-        hid = buf([P, 4, P, 4], BF16, "hid")
+        hid = buf([P, 4, S], BF16, "hid")
         ye = []
         re = []
         for c in range(4):
             ye.append(bank(4 + c, "ye%d" % c))
             for t in range(4):
                 weight_pass(ye[c][:, P * t : P * (t + 1)], w3, t, eq, eq_s, slice(P * c, P * (c + 1)))
-        for c in range(4):
-            re.append(bank(c, "re%d" % c))
-            for t in range(4):
-                weight_pass(re[c][:, P * t : P * (t + 1)], w1, t, xq, xq_s, slice(P * c, P * (c + 1)))
         picked = []
-        for c in range(4):
-            picked.append(buf([P, 4, P], F32, "picked%d" % c))
-            for t in range(4):
-                window = gate[t][:].indirect(pol_t[:, 8 * c : 8 * (c + 1)])
-                nc.scalar.activation(picked[c][:, t, :], window, ACT.Copy)
+        for t in range(4):
+            re.append(bank(t, "re%d" % t))
+            weight_pass(re[t][:], w1, t, xq, xq_s, slice(0, S))
+            picked.append(buf([P, S], F32, "picked%d" % t))
+            for h in range(2):
+                nc.scalar.activation(picked[t][:, H * h : H * (h + 1)], th[t][:].indirect(pol_t[:, 16 * h : 16 * (h + 1)]),
+                                     ACT.Copy, bias=0.4)
         warm = buf([P, 1], F32, "warm")
-        nc.scalar.activation(warm[:], picked[3][:, 3, P - 1 : P], ACT.Abs_reciprocal_sqrt, bias=units[:, 0:1])
+        nc.scalar.activation(warm[:], picked[3][:, S - 1 : S], ACT.Abs_reciprocal_sqrt, bias=units[:, 0:1])
         for c in range(4):
             nc.vector.tensor_tensor(
                 hid2[:, P * c : P * (c + 1), :],
@@ -186,22 +181,18 @@ def tile_picked_ybeamsl_sat_po_kernel(
         nc.vector.tensor_copy(floor[:], noise_ps[:, 0:S:P])
         h2q = buf([P, S], U32, "h2q")
         h2s = buf([P, S], U8, "h2s")
-        for c in range(4):
-            nc.vector.tensor_tensor(
-                hid[:, :, 32 * c : 32 * (c + 1), :].rearrange("p r m t -> p m t r"),
-                re[c][:].rearrange("p (t m r) -> p m t r", t=4, r=4),
-                picked[c][:].rearrange("p t (m r) -> p m t r", r=4),
-                ALU.mult,
-            )
-            if c == 0:
-                nc.vector.quantize_mx(out=h2q[:].bitcast(FP8X4), scales=h2s[:], in_=hid2[:].rearrange("p n t -> p (n t)"))
+        nc.vector.quantize_mx(out=h2q[:].bitcast(FP8X4), scales=h2s[:], in_=hid2[:].rearrange("p n t -> p (n t)"))
+        for t in range(4):
+            nc.vector.scalar_tensor_tensor(hid[:, t, :], re[t][:], units[:, t : t + 1], picked[t][:], ALU.mult, ALU.mult)
 
         sc = []
         power = []
         for r in range(4):
+            dealt = buf([P, P, 4], BF16, "dealt%d" % r)
+            nc.vector.tensor_copy(dealt[:], hid[:].rearrange("p t (m r) -> p r m t", r=4)[:, r])
             hq = buf([P, P], U32, "hq%d" % r)
             hs = buf([P, P], U8, "hs%d" % r)
-            nc.vector.quantize_mx(out=hq[:].bitcast(FP8X4), scales=hs[:], in_=hid[:, r].rearrange("p m t -> p (m t)"))
+            nc.vector.quantize_mx(out=hq[:].bitcast(FP8X4), scales=hs[:], in_=dealt[:].rearrange("p m t -> p (m t)"))
             sc.append(bank(4 + r, "sc%d" % r))
             nc.tensor.matmul_mx(
                 out=sc[r][:], lhsT=hq[:].bitcast(FP8X4), lhsT_scale=hs[:],

@@ -1,3 +1,4 @@
+import math
 from contextlib import ExitStack
 
 import concourse.mybir as mybir
@@ -85,34 +86,28 @@ def tile_picked_ybeamsl_sat_po_kernel(
             )
 
         xs = scale_tile(STORE, "xs", nc.gpsimd)
-        w2s = scale_tile(S, "w2s", nc.gpsimd)
-        load_scales(w2s, w2_scales, [nc.gpsimd], 3)
         unit_rows = buf([P, P], F32, "unit_rows")
         nc.gpsimd.memset(unit_rows[:], 0.0)
+        ident = buf([P, P], F32, "ident")
+        make_identity(nc, ident[:])
         for a, u in enumerate((unit, unit2)):
             nc.gpsimd.dma_start(
                 unit_rows[4 * a : 4 * a + 4, :].rearrange("t (b r) -> t b r", r=8),
                 u.rearrange("(b t r) o -> t b (r o)", t=4, r=8),
             )
-        ident = buf([P, P], F32, "ident")
-        make_identity(nc, ident[:])
-        leak = buf([P, H], F32, "leak")
-        nc.vector.memset(leak[:], 0.75)
-        noise = buf([P, STORE], F32, "noise")
-        nc.vector.memset(noise[:], 0.0)
+        w2s = scale_tile(S, "w2s", nc.vector)
         es = scale_tile(STORE, "es", nc.vector)
         w3s = scale_tile(S, "w3s", nc.vector)
         w1s = scale_tile(S, "w1s", nc.vector)
 
         load_scales(xs, x_scales, (nc.scalar, nc.sync, nc.sync, nc.sync))
         warm_tanh = buf([P, 1], F32, "warm_tanh")
-        nc.scalar.activation(warm_tanh[:], leak[:, 0:1], ACT.Tanh)
+        nc.scalar.activation(warm_tanh[:], ident[:, 0:1], ACT.Tanh)
         offs_t = load_list(offs, "offs_t")
         xw = load_words(x_words, "xw")
         txb_t = load_list(txb, "txb_t")
         w2w = load_fp4(w2_words, "w2w")
-        nc.sync.dma_start(noise[0:1, :], noi[0:1, :])
-        load_scales(w2s, w2_scales, [nc.sync] * 3)
+        load_scales(w2s, w2_scales, [nc.sync] * 4)
         ew = load_words(e_words, "ew")
         load_scales(es, e_scales, [nc.sync] * 4)
         w3w = load_fp4(w3_words, "w3w")
@@ -120,6 +115,8 @@ def tile_picked_ybeamsl_sat_po_kernel(
         pol_t = load_list(pol, "pol_t")
         w1w = load_fp4(w1_words, "w1w")
         load_scales(w1s, w1_scales, [nc.sync] * 4)
+        noise = buf([P, STORE], F32, "noise")
+        nc.sync.dma_start(noise[:], noi)
         adj_t = load_list(adj, "adj_t")
 
         xq_s = buf([P, S], U8, "xq_s")
@@ -128,8 +125,6 @@ def tile_picked_ybeamsl_sat_po_kernel(
         nc.vector.tensor_copy(xq[:], xw[:].indirect(offs_t[:]))
         w2 = deal(w2w, w2s, "w2", nc.vector)
 
-        noise_rows = buf([P, S], F32, "noise_rows")
-        nc.scalar.activation(noise_rows[:], noise[:].indirect(txb_t[:]), ACT.Copy, bias=0.3, scale=1.5)
 
         th = []
         for t in range(4):
@@ -142,11 +137,11 @@ def tile_picked_ybeamsl_sat_po_kernel(
         nc.vector.tensor_copy(eq[:], ew[:].indirect(txb_t[:]))
         eq_s = buf([P, S], U8, "eq_s")
         nc.vector.tensor_copy(eq_s[:], es[:].indirect(txb_t[:]))
+        w3 = deal(w3w, w3s, "w3", nc.vector)
         unit_ps = bank(0, "unit_ps")
         nc.tensor.transpose(unit_ps[:, 0:P], unit_rows[:], ident[:])
-        units = buf([P, 8], F32, "units", "es")
+        units = buf([P, 8], F32, "units", "w3s")
         nc.vector.tensor_copy(units[:], unit_ps[:, 0:8])
-        w3 = deal(w3w, w3s, "w3", nc.gpsimd)
         w1 = deal(w1w, w1s, "w1", nc.gpsimd)
 
         hid2 = buf([P, S, 4], BF16, "hid2")
@@ -165,8 +160,10 @@ def tile_picked_ybeamsl_sat_po_kernel(
             for h in range(2):
                 nc.scalar.activation(picked[t][:, H * h : H * (h + 1)], th[t][:].indirect(pol_t[:, 16 * h : 16 * (h + 1)]),
                                      ACT.Copy, bias=0.4)
+        noise_rows = buf([P, S], F32, "noise_rows", "th3")
+        nc.scalar.activation(noise_rows[:], noise[:].indirect(txb_t[:]), ACT.Copy, bias=0.3, scale=1.5)
         warm = buf([P, 1], F32, "warm")
-        nc.scalar.activation(warm[:], picked[3][:, S - 1 : S], ACT.Abs_reciprocal_sqrt, bias=units[:, 0:1])
+        nc.scalar.activation(warm[:], noise_rows[:, S - 1 : S], ACT.Abs_reciprocal_sqrt)
         for c in range(4):
             nc.vector.tensor_tensor(
                 hid2[:, P * c : P * (c + 1), :],
@@ -174,16 +171,17 @@ def tile_picked_ybeamsl_sat_po_kernel(
                 units[:, 4:8].unsqueeze(1).to_broadcast([P, P, 4]),
                 ALU.mult,
             )
-        noise_ps = bank(4, "noise_ps")
-        for c in range(4):
-            nc.tensor.transpose(noise_ps[:, P * c : P * (c + 1)], noise_rows[:, P * c : P * (c + 1)], ident[:])
-        floor = buf([P, 4], F32, "floor")
-        nc.vector.tensor_copy(floor[:], noise_ps[:, 0:S:P])
         h2q = buf([P, S], U32, "h2q")
         h2s = buf([P, S], U8, "h2s")
         nc.vector.quantize_mx(out=h2q[:].bitcast(FP8X4), scales=h2s[:], in_=hid2[:].rearrange("p n t -> p (n t)"))
         for t in range(4):
             nc.vector.scalar_tensor_tensor(hid[:, t, :], re[t][:], units[:, t : t + 1], picked[t][:], ALU.mult, ALU.mult)
+
+        noise_ps = bank(0, "noise_ps")
+        for c in range(4):
+            nc.tensor.transpose(noise_ps[:, P * c : P * (c + 1)], noise_rows[:, P * c : P * (c + 1)], ident[:])
+        floor = buf([P, 4], F32, "floor")
+        nc.scalar.copy(floor[:], noise_ps[:, 0:S:P])
 
         sc = []
         power = []
@@ -199,59 +197,65 @@ def tile_picked_ybeamsl_sat_po_kernel(
                 rhs=h2q[:].bitcast(FP8X4), rhs_scale=h2s[:], start=True, stop=True,
             )
             power.append(buf([P, S], F32, "power%d" % r))
-            nc.scalar.activation(power[r][:], sc[r][:], ACT.Square)
+            nc.scalar.activation(power[r][:], sc[r][:], ACT.Square, scale=math.sqrt(0.75))
 
         out_rows = out_0.rearrange("(p r) e -> p r e", r=4)
         oq = buf([P, S], U32, "oq")
         osc = buf([P, S], U8, "osc")
         result = [buf([P, 4, H], F32, "result%d" % h) for h in range(2)]
-        groups = [[(0,0)],[(1,0)],[(0,1),(1,1)],[(0,2),(0,3)],[(1,2),(1,3)]]
-        accs = {}
+        pieces = [(0, 0), (1, 0), (0, 1), (1, 1), (0, 2), (0, 3), (1, 2), (1, 3)]
+        inv = {}
+        den = {}
 
         def front(g):
-            acc = bank(g % 2, "acc%d" % g)
-            accs[g] = acc
-            for k, (h, r) in enumerate(groups[g]):
-                leaked = buf([P, H], F32, "leaked%d%d" % (h, r), "")
-                window = power[r][:].indirect(adj_t[:, 16 * h : 16 * (h + 1)])
-                if True:
-                    nc.vector.tensor_tensor(leaked[:], window, leak[:], ALU.mult)
-                else:
-                    nc.scalar.activation(leaked[:], window, ACT.Copy, scale=0.75)
+            h, r = pieces[g]
+            cols = slice(H * h, H * (h + 1))
+            window = power[r][:].indirect(adj_t[:, 16 * h : 16 * (h + 1)])
+            if g in (2, 4):
+                leaked = buf([P, H], F32, "leaked%d" % g, "")
+                nc.scalar.activation(leaked[:], window, ACT.Copy, scale=0.75)
+                den[g] = bank(g % 2, "den%d" % g)
                 for b in range(0, H, P):
-                    cols = slice(H * k + b, H * k + b + P)
-                    nc.tensor.matmul(acc[:, cols], power[r][:, H * h + b : H * h + b + P], ident[:],
+                    nc.tensor.matmul(den[g][:, b : b + P], power[r][:, H * h + b : H * h + b + P], ident[:],
                                      start=True, stop=False, is_transpose=True)
-                    nc.tensor.matmul(acc[:, cols], leaked[:, b : b + P], ident[:], start=False, stop=True, is_transpose=True)
+                    nc.tensor.matmul(den[g][:, b : b + P], leaked[:, b : b + P], ident[:], start=False, stop=True, is_transpose=True)
+                return
+            own = buf([P, H], F32, "own%d" % g)
+            nc.vector.scalar_tensor_tensor(own[:], power[r][:, cols], 4.0 / 3.0, noise_rows[:, cols], ALU.mult, ALU.add)
+            den[g] = buf([P, H], F32, "den%d" % g)
+            if True:
+                nc.vector.tensor_tensor(den[g][:], window, own[:], ALU.add)
+            else:
+                leaked = buf([P, H], F32, "leaked%d" % g, "")
+                nc.scalar.activation(leaked[:], window, ACT.Copy)
+                nc.vector.tensor_tensor(den[g][:], leaked[:], own[:], ALU.add)
 
         def middle(g):
-            acc = accs[g]
-            width = H * len(groups[g])
-            root = buf([P, width], F32, "root%d" % g, "")
-            for j in sorted(set(2 * h + b for h, r in groups[g] for b in range(2))):
-                ks = [k for k, (h, r) in enumerate(groups[g]) if h == j // 2]
-                nc.scalar.activation(root[:].rearrange("p (k b n) -> p k b n", b=2, n=P)[:, ks[0] : ks[-1] + 1, j % 2, :],
-                                     acc[:, 0:width].rearrange("p (k b n) -> p k b n", b=2, n=P)[:, ks[0] : ks[-1] + 1, j % 2, :],
-                                     ACT.Abs_reciprocal_sqrt, bias=floor[:, j : j + 1])
-            inv = buf([P, width], F32, "inv%d" % g)
-            nc.scalar.activation(inv[:], root[:], ACT.Square)
-            if True:
-                acc = bank(2 + g % 2, "back%d" % g)
-                accs[g] = acc
-            for b in range(0, width, P):
-                nc.tensor.transpose(acc[:, b : b + P], inv[:, b : b + P], ident[:])
+            h, r = pieces[g]
+            root = buf([P, H], F32, "root%d" % g)
+            square = buf([P, H], F32, "inv%d" % g)
+            if g in (2, 4):
+                for b in range(2):
+                    nc.scalar.activation(root[:, P * b : P * (b + 1)], den[g][:, P * b : P * (b + 1)], ACT.Abs_reciprocal_sqrt,
+                                         bias=floor[:, 2 * h + b : 2 * h + b + 1], scale=4.0 / 3.0)
+                nc.scalar.activation(square[:], root[:], ACT.Square)
+                inv[g] = bank(2 + g % 2, "back%d" % g)
+                for b in range(0, H, P):
+                    nc.tensor.transpose(inv[g][:, b : b + P], square[:, b : b + P], ident[:])
+                return
+            nc.scalar.activation(root[:], den[g][:], ACT.Abs_reciprocal_sqrt)
+            nc.scalar.activation(square[:], root[:], ACT.Square)
+            inv[g] = square
 
         def back(g):
-            shares = []
-            for k, (h, r) in enumerate(groups[g]):
-                shares.append(buf([P, H], F32, "share%d%d" % (h, r)))
-                nc.vector.tensor_tensor(shares[k][:], accs[g][:, H * k : H * (k + 1)], power[r][:, H * h : H * (h + 1)], ALU.mult)
-            for k, (h, r) in enumerate(groups[g]):
-                cols = slice(H * h, H * (h + 1))
-                nc.vector.tensor_tensor(result[h][:, r, :], sc[r][:, cols], shares[k][:], ALU.mult)
-                nc.sync.dma_start(out_rows[:, r, cols], result[h][:, r, :])
-                if r == 3 and h == 0:
-                    round_cols(nc.scalar.copy, 0, 0, H)
+            h, r = pieces[g]
+            cols = slice(H * h, H * (h + 1))
+            share = buf([P, H], F32, "share%d" % g)
+            nc.vector.tensor_tensor(share[:], inv[g][:, 0:H], power[r][:, cols], ALU.mult)
+            nc.vector.scalar_tensor_tensor(result[h][:, r, :], sc[r][:, cols], 4.0 / 3.0, share[:], ALU.mult, ALU.mult)
+            nc.sync.dma_start(out_rows[:, r, cols], result[h][:, r, :])
+            if r == 3 and h == 0:
+                round_cols(nc.scalar.copy, 0, 0, H)
 
         rounded = {}
 
@@ -269,7 +273,7 @@ def tile_picked_ybeamsl_sat_po_kernel(
             cols = slice(H * h, H * (h + 1))
             nc.sync.dma_start(out_1[0].rearrange("p n t -> p (n t)").bitcast(I32)[:, cols], oq[:, cols].bitcast(I32))
 
-        n = len(groups)
+        n = len(pieces)
         for step in range(n + 3):
             if step < n:
                 front(step)

@@ -18,8 +18,12 @@ ALU = mybir.AluOpType
 P = 128
 S = 512
 STORE = 1024
-H = 256
+HALF = 256
+LEAK = 0.75
 FLOPS = 4 * 2 * 512 * 512 * 512
+
+PIECES = [(0, 0), (1, 0), (0, 1), (1, 1), (0, 2), (0, 3), (1, 2), (1, 3)]
+TENSOR_PIECES = [(0, 1), (0, 2)]
 
 
 def tile_picked_ybeamsl_sat_po_kernel(
@@ -31,139 +35,149 @@ def tile_picked_ybeamsl_sat_po_kernel(
         sb = ctx.enter_context(tc.tile_pool(name="sb", bufs=1))
         ps = ctx.enter_context(tc.psum_pool(name="ps", bufs=1))
 
-        def buf(shape, dtype, name, tag=""):
-            return sb.tile(shape, dtype, name=name, tag=tag or name, align_bytes=64)
+        def buf(shape, dtype, name, reuses=""):
+            return sb.tile(shape, dtype, name=name, tag=reuses or name, align_bytes=64)
 
         def bank(b, name):
             return ps.tile([P, S], F32, name=name, tag="bank%d" % b)
 
+        def half(h):
+            return slice(HALF * h, HALF * (h + 1))
+
         def load_list(src, name):
-            t = sb.tile([P, S // 16], U16, name=name)
-            nc.sync.dma_start(t[:], src)
-            return t
+            offsets = sb.tile([P, S // 16], U16, name=name)
+            nc.sync.dma_start(offsets[:], src)
+            return offsets
+
+        def list_half(offsets, h):
+            return offsets[:, 16 * h : 16 * (h + 1)]
 
         def scale_tile(width, name, engine):
-            t = buf([P, width], U8, name)
-            engine.memset(t[:].bitcast(I32), 0)
-            return t
+            scales = buf([P, width], U8, name)
+            engine.memset(scales[:].bitcast(I32), 0)
+            return scales
 
-        def load_scales(t, src, queues, first=0):
-            for q, queue in enumerate(queues, first):
-                queue.dma_start(t[32 * q : 32 * q + 4, :].bitcast(I32), src[0, 4 * q : 4 * q + 4, :].bitcast(I32))
+        def load_scales(scales, src, first_queue):
+            for q in range(4):
+                queue = first_queue if q == 0 else nc.sync
+                queue.dma_start(scales[32 * q : 32 * q + 4, :].bitcast(I32), src[0, 4 * q : 4 * q + 4, :].bitcast(I32))
 
-        def load_words(src, name):
-            t = buf([P, STORE], U32, name)
-            nc.sync.dma_start(t[:].bitcast(I32), src[0].rearrange("p n t -> p (n t)").bitcast(I32))
-            return t
+        def load_e4m3(src, name):
+            words = buf([P, STORE], U32, name)
+            nc.sync.dma_start(words[:].bitcast(I32), src[0].rearrange("p n t -> p (n t)").bitcast(I32))
+            return words
 
-        def load_fp4(src, name):
-            t = buf([P, 2 * S], U8, name)
-            nc.sync.dma_start(t[:].bitcast(I32), src[0].bitcast(I32))
-            return t
+        def load_e2m1(src, name):
+            words = buf([P, 2 * S], U8, name)
+            nc.sync.dma_start(words[:].bitcast(I32), src[0].bitcast(I32))
+            return words
 
         def deal(words, scales, name, engine):
-            dw = buf([P, 2 * S], U8, name + "_dw")
-            ds = buf([P, S], U8, name + "_ds")
+            dealt_words = buf([P, 2 * S], U8, name + "_dealt_words")
+            dealt_scales = buf([P, S], U8, name + "_dealt_scales")
             engine.tensor_copy(
-                dw[:].bitcast(I32).rearrange("p (t b j) -> p t b j", t=4, j=4),
+                dealt_words[:].bitcast(I32).rearrange("p (t b j) -> p t b j", t=4, j=4),
                 words[:].bitcast(I32).rearrange("p (b t j) -> p t b j", t=4, j=4),
             )
             engine.tensor_copy(
-                ds[:].bitcast(I32).rearrange("p (t b j) -> p t b j", t=4, j=2),
+                dealt_scales[:].bitcast(I32).rearrange("p (t b j) -> p t b j", t=4, j=2),
                 scales[:].bitcast(I32).rearrange("p (b t j) -> p t b j", t=4, j=2),
             )
-            return dw, ds
+            return dealt_words, dealt_scales
 
-        def weight_pass(out, w, t, codes, scales, cols):
+        def weight_pass(out, weight, t, codes, scales, cols):
             nc.tensor.matmul_mx(
                 out=out,
-                lhsT=w[0][:, 256 * t : 256 * (t + 1)].bitcast(FP4X4),
-                lhsT_scale=w[1][:, P * t : P * (t + 1)],
+                lhsT=weight[0][:, 2 * P * t : 2 * P * (t + 1)].bitcast(FP4X4),
+                lhsT_scale=weight[1][:, P * t : P * (t + 1)],
                 rhs=codes[:, cols].bitcast(FP8X4),
                 rhs_scale=scales[:, cols],
                 start=True,
                 stop=True,
             )
 
-        xs = scale_tile(STORE, "xs", nc.gpsimd)
+        def quantize(codes, scales, values):
+            nc.vector.quantize_mx(out=codes.bitcast(FP8X4), scales=scales, in_=values.rearrange("p n t -> p (n t)"))
+
+        def interleave(copy, out, planes):
+            copy(out.rearrange("p (c i) t -> p c t i", i=4), planes.rearrange("p t (c i) -> p c t i", i=4))
+
+        x_scale_store = scale_tile(STORE, "x_scale_store", nc.gpsimd)
         unit_rows = buf([P, P], F32, "unit_rows")
         nc.gpsimd.memset(unit_rows[:], 0.0)
         ident = buf([P, P], F32, "ident")
         make_identity(nc, ident[:])
-        for a, u in enumerate((unit, unit2)):
+        for which, factors in enumerate((unit, unit2)):
             nc.gpsimd.dma_start(
-                unit_rows[4 * a : 4 * a + 4, :].rearrange("t (b r) -> t b r", r=8),
-                u.rearrange("(b t r) o -> t b (r o)", t=4, r=8),
+                unit_rows[4 * which : 4 * which + 4, :].rearrange("t (b a) -> t b a", a=8),
+                factors.rearrange("(b t a) o -> t b (a o)", t=4, a=8),
             )
-        w2s = scale_tile(S, "w2s", nc.vector)
-        es = scale_tile(STORE, "es", nc.vector)
-        w3s = scale_tile(S, "w3s", nc.vector)
-        w1s = scale_tile(S, "w1s", nc.vector)
+        w2_scale_rows = scale_tile(S, "w2_scale_rows", nc.vector)
+        e_scale_store = scale_tile(STORE, "e_scale_store", nc.vector)
+        w3_scale_rows = scale_tile(S, "w3_scale_rows", nc.vector)
+        w1_scale_rows = scale_tile(S, "w1_scale_rows", nc.vector)
 
-        load_scales(xs, x_scales, (nc.scalar, nc.sync, nc.sync, nc.sync))
-        warm_tanh = buf([P, 1], F32, "warm_tanh")
-        nc.scalar.activation(warm_tanh[:], ident[:, 0:1], ACT.Tanh)
-        offs_t = load_list(offs, "offs_t")
-        xw = load_words(x_words, "xw")
-        txb_t = load_list(txb, "txb_t")
-        w2w = load_fp4(w2_words, "w2w")
-        load_scales(w2s, w2_scales, [nc.sync] * 4)
-        ew = load_words(e_words, "ew")
-        load_scales(es, e_scales, [nc.sync] * 4)
-        w3w = load_fp4(w3_words, "w3w")
-        load_scales(w3s, w3_scales, [nc.sync] * 4)
-        pol_t = load_list(pol, "pol_t")
-        w1w = load_fp4(w1_words, "w1w")
-        load_scales(w1s, w1_scales, [nc.sync] * 4)
-        noise = buf([P, STORE], F32, "noise")
-        nc.sync.dma_start(noise[:], noi)
-        adj_t = load_list(adj, "adj_t")
+        load_scales(x_scale_store, x_scales, nc.scalar)
+        tanh_warmup = buf([P, 1], F32, "tanh_warmup")
+        nc.scalar.activation(tanh_warmup[:], ident[:, 0:1], ACT.Tanh)
+        offs_list = load_list(offs, "offs_list")
+        x_store = load_e4m3(x_words, "x_store")
+        txb_list = load_list(txb, "txb_list")
+        w2_raw = load_e2m1(w2_words, "w2_raw")
+        load_scales(w2_scale_rows, w2_scales, nc.sync)
+        e_store = load_e4m3(e_words, "e_store")
+        load_scales(e_scale_store, e_scales, nc.sync)
+        w3_raw = load_e2m1(w3_words, "w3_raw")
+        load_scales(w3_scale_rows, w3_scales, nc.sync)
+        pol_list = load_list(pol, "pol_list")
+        w1_raw = load_e2m1(w1_words, "w1_raw")
+        load_scales(w1_scale_rows, w1_scales, nc.sync)
+        noise_store = buf([P, STORE], F32, "noise_store")
+        nc.sync.dma_start(noise_store[:], noi)
+        adj_list = load_list(adj, "adj_list")
 
-        xq_s = buf([P, S], U8, "xq_s")
-        nc.vector.tensor_copy(xq_s[:], xs[:].indirect(offs_t[:]))
-        xq = buf([P, S], U32, "xq")
-        nc.vector.tensor_copy(xq[:], xw[:].indirect(offs_t[:]))
-        w2 = deal(w2w, w2s, "w2", nc.vector)
-
-
-        th = []
+        x_picked_scales = buf([P, S], U8, "x_picked_scales")
+        nc.vector.tensor_copy(x_picked_scales[:], x_scale_store[:].indirect(offs_list[:]))
+        x_picked = buf([P, S], U32, "x_picked")
+        nc.vector.tensor_copy(x_picked[:], x_store[:].indirect(offs_list[:]))
+        w2 = deal(w2_raw, w2_scale_rows, "w2", nc.vector)
+        tanh_im = []
         for t in range(4):
-            im = bank(t, "im%d" % t)
-            weight_pass(im[:], w2, t, xq, xq_s, slice(0, S))
-            th.append(buf([P, S], F32, "th%d" % t, ""))
-            nc.scalar.activation(th[t][:], im[:], ACT.Tanh)
+            im2 = bank(t, "im2_%d" % t)
+            weight_pass(im2[:], w2, t, x_picked, x_picked_scales, slice(0, S))
+            tanh_im.append(buf([P, S], F32, "tanh_im%d" % t))
+            nc.scalar.activation(tanh_im[t][:], im2[:], ACT.Tanh)
 
-        eq = buf([P, S], U32, "eq")
-        nc.vector.tensor_copy(eq[:], ew[:].indirect(txb_t[:]))
-        eq_s = buf([P, S], U8, "eq_s")
-        nc.vector.tensor_copy(eq_s[:], es[:].indirect(txb_t[:]))
-        w3 = deal(w3w, w3s, "w3", nc.vector)
-        unit_ps = bank(0, "unit_ps")
-        nc.tensor.transpose(unit_ps[:, 0:P], unit_rows[:], ident[:])
-        units = buf([P, 8], F32, "units", "w3s")
-        nc.vector.tensor_copy(units[:], unit_ps[:, 0:8])
-        w1 = deal(w1w, w1s, "w1", nc.gpsimd)
+        e_picked = buf([P, S], U32, "e_picked")
+        nc.vector.tensor_copy(e_picked[:], e_store[:].indirect(txb_list[:]))
+        e_picked_scales = buf([P, S], U8, "e_picked_scales")
+        nc.vector.tensor_copy(e_picked_scales[:], e_scale_store[:].indirect(txb_list[:]))
+        w3 = deal(w3_raw, w3_scale_rows, "w3", nc.vector)
+        units_psum = bank(0, "units_psum")
+        nc.tensor.transpose(units_psum[:, 0:P], unit_rows[:], ident[:])
+        units = buf([P, 8], F32, "units", reuses="w3_scale_rows")
+        nc.vector.tensor_copy(units[:], units_psum[:, 0:8])
+        w1 = deal(w1_raw, w1_scale_rows, "w1", nc.gpsimd)
 
         hid2 = buf([P, S, 4], BF16, "hid2")
-        hid = buf([P, 4, S], BF16, "hid")
+        hid = buf([P, 4, 4, P], BF16, "hid")
         ye = []
-        re = []
         for c in range(4):
             ye.append(bank(4 + c, "ye%d" % c))
             for t in range(4):
-                weight_pass(ye[c][:, P * t : P * (t + 1)], w3, t, eq, eq_s, slice(P * c, P * (c + 1)))
-        picked = []
+                weight_pass(ye[c][:, P * t : P * (t + 1)], w3, t, e_picked, e_picked_scales, slice(P * c, P * (c + 1)))
+        re = []
+        gate = []
         for t in range(4):
             re.append(bank(t, "re%d" % t))
-            weight_pass(re[t][:], w1, t, xq, xq_s, slice(0, S))
-            picked.append(buf([P, S], F32, "picked%d" % t))
+            weight_pass(re[t][:], w1, t, x_picked, x_picked_scales, slice(0, S))
+            gate.append(buf([P, S], F32, "gate%d" % t))
             for h in range(2):
-                nc.scalar.activation(picked[t][:, H * h : H * (h + 1)], th[t][:].indirect(pol_t[:, 16 * h : 16 * (h + 1)]),
-                                     ACT.Copy, bias=0.4)
-        noise_rows = buf([P, S], F32, "noise_rows", "th3")
-        nc.scalar.activation(noise_rows[:], noise[:].indirect(txb_t[:]), ACT.Copy, bias=0.3, scale=1.5)
-        warm = buf([P, 1], F32, "warm")
-        nc.scalar.activation(warm[:], noise_rows[:, S - 1 : S], ACT.Abs_reciprocal_sqrt)
+                nc.scalar.activation(gate[t][:, half(h)], tanh_im[t][:].indirect(list_half(pol_list, h)), ACT.Copy, bias=0.4)
+        floor_rows = buf([P, S], F32, "floor_rows", reuses="tanh_im3")
+        nc.scalar.activation(floor_rows[:], noise_store[:].indirect(txb_list[:]), ACT.Copy, bias=0.3, scale=1.5)
+        root_warmup = buf([P, 1], F32, "root_warmup")
+        nc.scalar.activation(root_warmup[:], floor_rows[:, S - 1 : S], ACT.Abs_reciprocal_sqrt)
         for c in range(4):
             nc.vector.tensor_tensor(
                 hid2[:, P * c : P * (c + 1), :],
@@ -171,123 +185,117 @@ def tile_picked_ybeamsl_sat_po_kernel(
                 units[:, 4:8].unsqueeze(1).to_broadcast([P, P, 4]),
                 ALU.mult,
             )
-        h2q = buf([P, S], U32, "h2q")
-        h2s = buf([P, S], U8, "h2s")
-        nc.vector.quantize_mx(out=h2q[:].bitcast(FP8X4), scales=h2s[:], in_=hid2[:].rearrange("p n t -> p (n t)"))
+        hid2_codes = buf([P, S], U32, "hid2_codes")
+        hid2_scales = buf([P, S], U8, "hid2_scales")
+        for h in range(2):
+            quantize(hid2_codes[:, half(h)], hid2_scales[:, half(h)], hid2[:, half(h), :])
         for t in range(4):
-            nc.vector.scalar_tensor_tensor(hid[:, t, :], re[t][:], units[:, t : t + 1], picked[t][:], ALU.mult, ALU.mult)
+            nc.vector.scalar_tensor_tensor(
+                hid[:, t].rearrange("p r m -> p m r"),
+                re[t][:].rearrange("p (m r) -> p m r", r=4),
+                units[:, t : t + 1],
+                gate[t][:].rearrange("p (m r) -> p m r", r=4),
+                ALU.mult,
+                ALU.mult,
+            )
 
-        noise_ps = bank(0, "noise_ps")
-        for c in range(4):
-            nc.tensor.transpose(noise_ps[:, P * c : P * (c + 1)], noise_rows[:, P * c : P * (c + 1)], ident[:])
-        floor = buf([P, 4], F32, "floor")
-        nc.scalar.copy(floor[:], noise_ps[:, 0:S:P])
+        floor_psum = bank(0, "floor_psum")
+        for c in range(HALF // P):
+            nc.tensor.transpose(floor_psum[:, P * c : P * (c + 1)], floor_rows[:, P * c : P * (c + 1)], ident[:])
+        floor_cols = buf([P, HALF // P], F32, "floor_cols")
+        nc.scalar.copy(floor_cols[:], floor_psum[:, 0:HALF:P])
 
         sc = []
-        power = []
+        leak = []
         for r in range(4):
-            dealt = buf([P, P, 4], BF16, "dealt%d" % r)
-            nc.vector.tensor_copy(dealt[:], hid[:].rearrange("p t (m r) -> p r m t", r=4)[:, r])
-            hq = buf([P, P], U32, "hq%d" % r)
-            hs = buf([P, P], U8, "hs%d" % r)
-            nc.vector.quantize_mx(out=hq[:].bitcast(FP8X4), scales=hs[:], in_=dealt[:].rearrange("p m t -> p (m t)"))
+            hid_rows = buf([P, P, 4], BF16, "hid_rows%d" % r)
+            interleave(nc.vector.tensor_copy, hid_rows[:], hid[:, :, r, :])
+            hid_codes = buf([P, P], U32, "hid_codes%d" % r)
+            hid_scales = buf([P, P], U8, "hid_scales%d" % r)
+            quantize(hid_codes[:], hid_scales[:], hid_rows[:])
             sc.append(bank(4 + r, "sc%d" % r))
             nc.tensor.matmul_mx(
-                out=sc[r][:], lhsT=hq[:].bitcast(FP8X4), lhsT_scale=hs[:],
-                rhs=h2q[:].bitcast(FP8X4), rhs_scale=h2s[:], start=True, stop=True,
+                out=sc[r][:], lhsT=hid_codes[:].bitcast(FP8X4), lhsT_scale=hid_scales[:],
+                rhs=hid2_codes[:].bitcast(FP8X4), rhs_scale=hid2_scales[:], start=True, stop=True,
             )
-            power.append(buf([P, S], F32, "power%d" % r))
-            nc.scalar.activation(power[r][:], sc[r][:], ACT.Square, scale=math.sqrt(0.75))
+            leak.append(buf([P, S], F32, "leak%d" % r))
+            nc.scalar.activation(leak[r][:], sc[r][:], ACT.Square, scale=math.sqrt(LEAK))
 
         out_rows = out_0.rearrange("(p r) e -> p r e", r=4)
-        oq = buf([P, S], U32, "oq")
-        osc = buf([P, S], U8, "osc")
-        result = [buf([P, 4, H], F32, "result%d" % h) for h in range(2)]
-        pieces = [(0, 0), (1, 0), (0, 1), (1, 1), (0, 2), (0, 3), (1, 2), (1, 3)]
-        inv = {}
+        out_codes = buf([P, S], U32, "out_codes")
+        out_scales = buf([P, S], U8, "out_scales")
+        result = [buf([P, 4, HALF], F32, "result%d" % h) for h in range(2)]
         den = {}
-
-        def front(g):
-            h, r = pieces[g]
-            cols = slice(H * h, H * (h + 1))
-            window = power[r][:].indirect(adj_t[:, 16 * h : 16 * (h + 1)])
-            if g in (2, 4):
-                leaked = buf([P, H], F32, "leaked%d" % g, "")
-                nc.scalar.activation(leaked[:], window, ACT.Copy, scale=0.75)
-                den[g] = bank(g % 2, "den%d" % g)
-                for b in range(0, H, P):
-                    nc.tensor.matmul(den[g][:, b : b + P], power[r][:, H * h + b : H * h + b + P], ident[:],
-                                     start=True, stop=False, is_transpose=True)
-                    nc.tensor.matmul(den[g][:, b : b + P], leaked[:, b : b + P], ident[:], start=False, stop=True, is_transpose=True)
-                return
-            own = buf([P, H], F32, "own%d" % g)
-            nc.vector.scalar_tensor_tensor(own[:], power[r][:, cols], 4.0 / 3.0, noise_rows[:, cols], ALU.mult, ALU.add)
-            den[g] = buf([P, H], F32, "den%d" % g)
-            if True:
-                nc.vector.tensor_tensor(den[g][:], window, own[:], ALU.add)
-            else:
-                leaked = buf([P, H], F32, "leaked%d" % g, "")
-                nc.scalar.activation(leaked[:], window, ACT.Copy)
-                nc.vector.tensor_tensor(den[g][:], leaked[:], own[:], ALU.add)
-
-        def middle(g):
-            h, r = pieces[g]
-            root = buf([P, H], F32, "root%d" % g)
-            square = buf([P, H], F32, "inv%d" % g)
-            if g in (2, 4):
-                for b in range(2):
-                    nc.scalar.activation(root[:, P * b : P * (b + 1)], den[g][:, P * b : P * (b + 1)], ACT.Abs_reciprocal_sqrt,
-                                         bias=floor[:, 2 * h + b : 2 * h + b + 1], scale=4.0 / 3.0)
-                nc.scalar.activation(square[:], root[:], ACT.Square)
-                inv[g] = bank(2 + g % 2, "back%d" % g)
-                for b in range(0, H, P):
-                    nc.tensor.transpose(inv[g][:, b : b + P], square[:, b : b + P], ident[:])
-                return
-            nc.scalar.activation(root[:], den[g][:], ACT.Abs_reciprocal_sqrt)
-            nc.scalar.activation(square[:], root[:], ACT.Square)
-            inv[g] = square
-
-        def back(g):
-            h, r = pieces[g]
-            cols = slice(H * h, H * (h + 1))
-            share = buf([P, H], F32, "share%d" % g)
-            nc.vector.tensor_tensor(share[:], inv[g][:, 0:H], power[r][:, cols], ALU.mult)
-            nc.vector.scalar_tensor_tensor(result[h][:, r, :], sc[r][:, cols], 4.0 / 3.0, share[:], ALU.mult, ALU.mult)
-            nc.sync.dma_start(out_rows[:, r, cols], result[h][:, r, :])
-            if r == 3 and h == 0:
-                round_cols(nc.scalar.copy, 0, 0, H)
-
+        inverse = {}
         rounded = {}
 
-        def round_cols(copy, h, c0, c1):
-            rounded[(h, c0)] = buf([P, c1 - c0, 4], BF16, "rounded%d_%d" % (h, c0))
-            copy(rounded[(h, c0)][:].rearrange("p (c i) r -> p c r i", i=4),
-                 result[h][:, :, c0:c1].rearrange("p r (c i) -> p c r i", i=4))
+        def sum_den(h, r):
+            window = leak[r][:].indirect(list_half(adj_list, h))
+            if (h, r) in TENSOR_PIECES:
+                adjacent = buf([P, HALF], F32, "adjacent%d%d" % (h, r))
+                nc.scalar.activation(adjacent[:], window, ACT.Copy, scale=LEAK)
+                den[h, r] = bank(0, "den%d%d" % (h, r))
+                for b in range(0, HALF, P):
+                    nc.tensor.matmul(den[h, r][:, b : b + P], leak[r][:, HALF * h + b : HALF * h + b + P], ident[:],
+                                     start=True, stop=False, is_transpose=True)
+                    nc.tensor.matmul(den[h, r][:, b : b + P], adjacent[:, b : b + P], ident[:],
+                                     start=False, stop=True, is_transpose=True)
+            else:
+                own = buf([P, HALF], F32, "own%d%d" % (h, r))
+                nc.vector.scalar_tensor_tensor(own[:], leak[r][:, half(h)], 1.0 / LEAK, floor_rows[:, half(h)],
+                                               ALU.mult, ALU.add)
+                den[h, r] = buf([P, HALF], F32, "den%d%d" % (h, r))
+                nc.vector.tensor_tensor(den[h, r][:], window, own[:], ALU.add)
 
-        def emit(h, c0, c1):
-            cols = slice(H * h + c0, H * h + c1)
-            nc.vector.quantize_mx(out=oq[:, cols].bitcast(FP8X4), scales=osc[:, cols],
-                                  in_=rounded[(h, c0)][:].rearrange("p e r -> p (e r)"))
+        def invert(h, r):
+            root = buf([P, HALF], F32, "root%d%d" % (h, r))
+            square = buf([P, HALF], F32, "square%d%d" % (h, r))
+            if (h, r) in TENSOR_PIECES:
+                for c in range(HALF // P):
+                    nc.scalar.activation(root[:, P * c : P * (c + 1)], den[h, r][:, P * c : P * (c + 1)],
+                                         ACT.Abs_reciprocal_sqrt, bias=floor_cols[:, c : c + 1], scale=1.0 / LEAK)
+                nc.scalar.activation(square[:], root[:], ACT.Square)
+                inverse[h, r] = bank(2, "inverse%d%d" % (h, r))
+                for b in range(0, HALF, P):
+                    nc.tensor.transpose(inverse[h, r][:, b : b + P], square[:, b : b + P], ident[:])
+            else:
+                nc.scalar.activation(root[:], den[h, r][:], ACT.Abs_reciprocal_sqrt)
+                nc.scalar.activation(square[:], root[:], ACT.Square)
+                inverse[h, r] = square
 
-        def store_words(h):
-            cols = slice(H * h, H * (h + 1))
-            nc.sync.dma_start(out_1[0].rearrange("p n t -> p (n t)").bitcast(I32)[:, cols], oq[:, cols].bitcast(I32))
+        def round_columns(copy, h, first, end):
+            rounded[h, first] = buf([P, end - first, 4], BF16, "rounded%d_%d" % (h, first))
+            interleave(copy, rounded[h, first][:], result[h][:, :, first:end])
 
-        n = len(pieces)
-        for step in range(n + 3):
-            if step < n:
-                front(step)
-            if 0 <= step - 1 < n:
-                middle(step - 1)
-            if 0 <= step - 2 < n:
-                back(step - 2)
-        round_cols(nc.vector.tensor_copy, 1, 0, P)
-        round_cols(nc.scalar.copy, 1, P, H)
-        emit(0, 0, H)
-        store_words(0)
-        emit(1, 0, P)
-        emit(1, P, H)
-        store_words(1)
+        def finish(h, r):
+            share = buf([P, HALF], F32, "share%d%d" % (h, r))
+            nc.vector.tensor_tensor(share[:], inverse[h, r][:, 0:HALF], leak[r][:, half(h)], ALU.mult)
+            nc.vector.scalar_tensor_tensor(result[h][:, r, :], sc[r][:, half(h)], 1.0 / LEAK, share[:], ALU.mult, ALU.mult)
+            nc.sync.dma_start(out_rows[:, r, half(h)], result[h][:, r, :])
+            if (h, r) == (0, 3):
+                round_columns(nc.scalar.copy, 0, 0, HALF)
+
+        def quantize_columns(h, first, end):
+            cols = slice(HALF * h + first, HALF * h + end)
+            quantize(out_codes[:, cols], out_scales[:, cols], rounded[h, first][:])
+
+        def store_codes(h):
+            words = out_1[0].rearrange("p n t -> p (n t)").bitcast(I32)
+            nc.sync.dma_start(words[:, half(h)], out_codes[:, half(h)].bitcast(I32))
+
+        steps = (sum_den, invert, finish)
+        for turn in range(len(PIECES) + len(steps) - 1):
+            for lag, step in enumerate(steps):
+                if 0 <= turn - lag < len(PIECES):
+                    step(*PIECES[turn - lag])
+
+        round_columns(nc.vector.tensor_copy, 1, 0, P)
+        round_columns(nc.scalar.copy, 1, P, HALF)
+        quantize_columns(0, 0, HALF)
+        store_codes(0)
+        quantize_columns(1, 0, P)
+        quantize_columns(1, P, HALF)
+        store_codes(1)
         for q in range(4):
             queue = nc.sync if q % 2 == 0 else nc.scalar
-            queue.dma_start(out_2[0, 4 * q : 4 * q + 4, :].bitcast(I32), osc[32 * q : 32 * q + 4, :].bitcast(I32))
+            queue.dma_start(out_2[0, 4 * q : 4 * q + 4, :].bitcast(I32), out_scales[32 * q : 32 * q + 4, :].bitcast(I32))

import math
from contextlib import ExitStack

import concourse.mybir as mybir
from concourse.masks import make_identity

F32 = mybir.dt.float32
BF16 = mybir.dt.bfloat16
I32 = mybir.dt.int32
U32 = mybir.dt.uint32
U16 = mybir.dt.uint16
U8 = mybir.dt.uint8
FP8X4 = mybir.dt.float8_e4m3fn_x4
FP4X4 = mybir.dt.float4_e2m1fn_x4
ACT = mybir.ActivationFunctionType
ALU = mybir.AluOpType

P = 128
S = 512
STORE = 1024
HALF = 256
LEAK = 0.75
FLOPS = 4 * 2 * 512 * 512 * 512

PIECES = [(0, 0), (1, 0), (0, 1), (1, 1), (0, 2), (0, 3), (1, 2), (1, 3)]
TENSOR_PIECES = [(0, 1), (0, 2)]


def tile_picked_ybeamsl_sat_po_kernel(
    tc, x_words, x_scales, w1_words, w1_scales, w2_words, w2_scales, e_words, e_scales,
    w3_words, w3_scales, unit, unit2, noi, offs, txb, pol, adj, out_0, out_1, out_2,
):
    nc = tc.nc
    with ExitStack() as ctx:
        sb = ctx.enter_context(tc.tile_pool(name="sb", bufs=1))
        ps = ctx.enter_context(tc.psum_pool(name="ps", bufs=1))

        def buf(shape, dtype, name, reuses=""):
            return sb.tile(shape, dtype, name=name, tag=reuses or name, align_bytes=64)

        def bank(b, name):
            return ps.tile([P, S], F32, name=name, tag="bank%d" % b)

        def half(h):
            return slice(HALF * h, HALF * (h + 1))

        def load_list(src, name):
            offsets = sb.tile([P, S // 16], U16, name=name)
            nc.sync.dma_start(offsets[:], src)
            return offsets

        def list_half(offsets, h):
            return offsets[:, 16 * h : 16 * (h + 1)]

        def scale_tile(width, name, engine):
            scales = buf([P, width], U8, name)
            engine.memset(scales[:].bitcast(I32), 0)
            return scales

        def load_scales(scales, src, first_queue):
            for q in range(4):
                queue = first_queue if q == 0 else nc.sync
                queue.dma_start(scales[32 * q : 32 * q + 4, :].bitcast(I32), src[0, 4 * q : 4 * q + 4, :].bitcast(I32))

        def load_e4m3(src, name):
            words = buf([P, STORE], U32, name)
            nc.sync.dma_start(words[:].bitcast(I32), src[0].rearrange("p n t -> p (n t)").bitcast(I32))
            return words

        def load_e2m1(src, name):
            words = buf([P, 2 * S], U8, name)
            nc.sync.dma_start(words[:].bitcast(I32), src[0].bitcast(I32))
            return words

        def deal(words, scales, name, engine):
            dealt_words = buf([P, 2 * S], U8, name + "_dealt_words")
            dealt_scales = buf([P, S], U8, name + "_dealt_scales")
            engine.tensor_copy(
                dealt_words[:].bitcast(I32).rearrange("p (t b j) -> p t b j", t=4, j=4),
                words[:].bitcast(I32).rearrange("p (b t j) -> p t b j", t=4, j=4),
            )
            engine.tensor_copy(
                dealt_scales[:].bitcast(I32).rearrange("p (t b j) -> p t b j", t=4, j=2),
                scales[:].bitcast(I32).rearrange("p (b t j) -> p t b j", t=4, j=2),
            )
            return dealt_words, dealt_scales

        def weight_pass(out, weight, t, codes, scales, cols):
            nc.tensor.matmul_mx(
                out=out,
                lhsT=weight[0][:, 2 * P * t : 2 * P * (t + 1)].bitcast(FP4X4),
                lhsT_scale=weight[1][:, P * t : P * (t + 1)],
                rhs=codes[:, cols].bitcast(FP8X4),
                rhs_scale=scales[:, cols],
                start=True,
                stop=True,
            )

        def quantize(codes, scales, values):
            nc.vector.quantize_mx(out=codes.bitcast(FP8X4), scales=scales, in_=values.rearrange("p n t -> p (n t)"))

        def interleave(copy, out, planes):
            copy(out.rearrange("p (c i) t -> p c t i", i=4), planes.rearrange("p t (c i) -> p c t i", i=4))

        x_scale_store = scale_tile(STORE, "x_scale_store", nc.gpsimd)
        unit_rows = buf([P, P], F32, "unit_rows")
        nc.gpsimd.memset(unit_rows[:], 0.0)
        ident = buf([P, P], F32, "ident")
        make_identity(nc, ident[:])
        for which, factors in enumerate((unit, unit2)):
            nc.gpsimd.dma_start(
                unit_rows[4 * which : 4 * which + 4, :].rearrange("t (b a) -> t b a", a=8),
                factors.rearrange("(b t a) o -> t b (a o)", t=4, a=8),
            )
        w2_scale_rows = scale_tile(S, "w2_scale_rows", nc.vector)
        e_scale_store = scale_tile(STORE, "e_scale_store", nc.vector)
        w3_scale_rows = scale_tile(S, "w3_scale_rows", nc.vector)
        w1_scale_rows = scale_tile(S, "w1_scale_rows", nc.vector)

        load_scales(x_scale_store, x_scales, nc.scalar)
        tanh_warmup = buf([P, 1], F32, "tanh_warmup")
        nc.scalar.activation(tanh_warmup[:], ident[:, 0:1], ACT.Tanh)
        offs_list = load_list(offs, "offs_list")
        x_store = load_e4m3(x_words, "x_store")
        txb_list = load_list(txb, "txb_list")
        w2_raw = load_e2m1(w2_words, "w2_raw")
        load_scales(w2_scale_rows, w2_scales, nc.sync)
        e_store = load_e4m3(e_words, "e_store")
        load_scales(e_scale_store, e_scales, nc.sync)
        w3_raw = load_e2m1(w3_words, "w3_raw")
        load_scales(w3_scale_rows, w3_scales, nc.sync)
        pol_list = load_list(pol, "pol_list")
        w1_raw = load_e2m1(w1_words, "w1_raw")
        load_scales(w1_scale_rows, w1_scales, nc.sync)
        noise_store = buf([P, STORE], F32, "noise_store")
        nc.sync.dma_start(noise_store[:], noi)
        adj_list = load_list(adj, "adj_list")

        x_picked_scales = buf([P, S], U8, "x_picked_scales")
        nc.vector.tensor_copy(x_picked_scales[:], x_scale_store[:].indirect(offs_list[:]))
        x_picked = buf([P, S], U32, "x_picked")
        nc.vector.tensor_copy(x_picked[:], x_store[:].indirect(offs_list[:]))
        w2 = deal(w2_raw, w2_scale_rows, "w2", nc.vector)
        tanh_im = []
        for t in range(4):
            im2 = bank(t, "im2_%d" % t)
            weight_pass(im2[:], w2, t, x_picked, x_picked_scales, slice(0, S))
            tanh_im.append(buf([P, S], F32, "tanh_im%d" % t))
            nc.scalar.activation(tanh_im[t][:], im2[:], ACT.Tanh)

        e_picked = buf([P, S], U32, "e_picked")
        nc.vector.tensor_copy(e_picked[:], e_store[:].indirect(txb_list[:]))
        e_picked_scales = buf([P, S], U8, "e_picked_scales")
        nc.vector.tensor_copy(e_picked_scales[:], e_scale_store[:].indirect(txb_list[:]))
        w3 = deal(w3_raw, w3_scale_rows, "w3", nc.vector)
        units_psum = bank(0, "units_psum")
        nc.tensor.transpose(units_psum[:, 0:P], unit_rows[:], ident[:])
        units = buf([P, 8], F32, "units", reuses="w3_scale_rows")
        nc.vector.tensor_copy(units[:], units_psum[:, 0:8])
        w1 = deal(w1_raw, w1_scale_rows, "w1", nc.gpsimd)

        hid2 = buf([P, S, 4], BF16, "hid2")
        hid = buf([P, 4, 4, P], BF16, "hid")
        ye = []
        for c in range(4):
            ye.append(bank(4 + c, "ye%d" % c))
            for t in range(4):
                weight_pass(ye[c][:, P * t : P * (t + 1)], w3, t, e_picked, e_picked_scales, slice(P * c, P * (c + 1)))
        re = []
        gate = []
        for t in range(4):
            re.append(bank(t, "re%d" % t))
            weight_pass(re[t][:], w1, t, x_picked, x_picked_scales, slice(0, S))
            gate.append(buf([P, S], F32, "gate%d" % t))
            for h in range(2):
                nc.scalar.activation(gate[t][:, half(h)], tanh_im[t][:].indirect(list_half(pol_list, h)), ACT.Copy, bias=0.4)
        floor_rows = buf([P, S], F32, "floor_rows", reuses="tanh_im3")
        nc.scalar.activation(floor_rows[:], noise_store[:].indirect(txb_list[:]), ACT.Copy, bias=0.3, scale=1.5)
        root_warmup = buf([P, 1], F32, "root_warmup")
        nc.scalar.activation(root_warmup[:], floor_rows[:, S - 1 : S], ACT.Abs_reciprocal_sqrt)
        for c in range(4):
            nc.vector.tensor_tensor(
                hid2[:, P * c : P * (c + 1), :],
                ye[c][:].rearrange("p (t n) -> p n t", t=4),
                units[:, 4:8].unsqueeze(1).to_broadcast([P, P, 4]),
                ALU.mult,
            )
        hid2_codes = buf([P, S], U32, "hid2_codes")
        hid2_scales = buf([P, S], U8, "hid2_scales")
        for h in range(2):
            quantize(hid2_codes[:, half(h)], hid2_scales[:, half(h)], hid2[:, half(h), :])
        for t in range(4):
            nc.vector.scalar_tensor_tensor(
                hid[:, t].rearrange("p r m -> p m r"),
                re[t][:].rearrange("p (m r) -> p m r", r=4),
                units[:, t : t + 1],
                gate[t][:].rearrange("p (m r) -> p m r", r=4),
                ALU.mult,
                ALU.mult,
            )

        floor_psum = bank(0, "floor_psum")
        for c in range(HALF // P):
            nc.tensor.transpose(floor_psum[:, P * c : P * (c + 1)], floor_rows[:, P * c : P * (c + 1)], ident[:])
        floor_cols = buf([P, HALF // P], F32, "floor_cols")
        nc.scalar.copy(floor_cols[:], floor_psum[:, 0:HALF:P])

        sc = []
        leak = []
        for r in range(4):
            hid_rows = buf([P, P, 4], BF16, "hid_rows%d" % r)
            interleave(nc.vector.tensor_copy, hid_rows[:], hid[:, :, r, :])
            hid_codes = buf([P, P], U32, "hid_codes%d" % r)
            hid_scales = buf([P, P], U8, "hid_scales%d" % r)
            quantize(hid_codes[:], hid_scales[:], hid_rows[:])
            sc.append(bank(4 + r, "sc%d" % r))
            nc.tensor.matmul_mx(
                out=sc[r][:], lhsT=hid_codes[:].bitcast(FP8X4), lhsT_scale=hid_scales[:],
                rhs=hid2_codes[:].bitcast(FP8X4), rhs_scale=hid2_scales[:], start=True, stop=True,
            )
            leak.append(buf([P, S], F32, "leak%d" % r))
            nc.scalar.activation(leak[r][:], sc[r][:], ACT.Square, scale=math.sqrt(LEAK))

        out_rows = out_0.rearrange("(p r) e -> p r e", r=4)
        out_codes = buf([P, S], U32, "out_codes")
        out_scales = buf([P, S], U8, "out_scales")
        result = [buf([P, 4, HALF], F32, "result%d" % h) for h in range(2)]
        den = {}
        inverse = {}
        rounded = {}

        def sum_den(h, r):
            window = leak[r][:].indirect(list_half(adj_list, h))
            if (h, r) in TENSOR_PIECES:
                adjacent = buf([P, HALF], F32, "adjacent%d%d" % (h, r))
                nc.scalar.activation(adjacent[:], window, ACT.Copy, scale=LEAK)
                den[h, r] = bank(0, "den%d%d" % (h, r))
                for b in range(0, HALF, P):
                    nc.tensor.matmul(den[h, r][:, b : b + P], leak[r][:, HALF * h + b : HALF * h + b + P], ident[:],
                                     start=True, stop=False, is_transpose=True)
                    nc.tensor.matmul(den[h, r][:, b : b + P], adjacent[:, b : b + P], ident[:],
                                     start=False, stop=True, is_transpose=True)
            else:
                own = buf([P, HALF], F32, "own%d%d" % (h, r))
                nc.vector.scalar_tensor_tensor(own[:], leak[r][:, half(h)], 1.0 / LEAK, floor_rows[:, half(h)],
                                               ALU.mult, ALU.add)
                den[h, r] = buf([P, HALF], F32, "den%d%d" % (h, r))
                nc.vector.tensor_tensor(den[h, r][:], window, own[:], ALU.add)

        def invert(h, r):
            root = buf([P, HALF], F32, "root%d%d" % (h, r))
            square = buf([P, HALF], F32, "square%d%d" % (h, r))
            if (h, r) in TENSOR_PIECES:
                for c in range(HALF // P):
                    nc.scalar.activation(root[:, P * c : P * (c + 1)], den[h, r][:, P * c : P * (c + 1)],
                                         ACT.Abs_reciprocal_sqrt, bias=floor_cols[:, c : c + 1], scale=1.0 / LEAK)
                nc.scalar.activation(square[:], root[:], ACT.Square)
                inverse[h, r] = bank(2, "inverse%d%d" % (h, r))
                for b in range(0, HALF, P):
                    nc.tensor.transpose(inverse[h, r][:, b : b + P], square[:, b : b + P], ident[:])
            else:
                nc.scalar.activation(root[:], den[h, r][:], ACT.Abs_reciprocal_sqrt)
                nc.scalar.activation(square[:], root[:], ACT.Square)
                inverse[h, r] = square

        def round_columns(copy, h, first, end):
            rounded[h, first] = buf([P, end - first, 4], BF16, "rounded%d_%d" % (h, first))
            interleave(copy, rounded[h, first][:], result[h][:, :, first:end])

        def finish(h, r):
            share = buf([P, HALF], F32, "share%d%d" % (h, r))
            nc.vector.tensor_tensor(share[:], inverse[h, r][:, 0:HALF], leak[r][:, half(h)], ALU.mult)
            nc.vector.scalar_tensor_tensor(result[h][:, r, :], sc[r][:, half(h)], 1.0 / LEAK, share[:], ALU.mult, ALU.mult)
            nc.sync.dma_start(out_rows[:, r, half(h)], result[h][:, r, :])
            if (h, r) == (0, 3):
                round_columns(nc.scalar.copy, 0, 0, HALF)

        def quantize_columns(h, first, end):
            cols = slice(HALF * h + first, HALF * h + end)
            quantize(out_codes[:, cols], out_scales[:, cols], rounded[h, first][:])

        def store_codes(h):
            words = out_1[0].rearrange("p n t -> p (n t)").bitcast(I32)
            nc.sync.dma_start(words[:, half(h)], out_codes[:, half(h)].bitcast(I32))

        steps = (sum_den, invert, finish)
        for turn in range(len(PIECES) + len(steps) - 1):
            for lag, step in enumerate(steps):
                if 0 <= turn - lag < len(PIECES):
                    step(*PIECES[turn - lag])

        round_columns(nc.vector.tensor_copy, 1, 0, P)
        round_columns(nc.scalar.copy, 1, P, HALF)
        quantize_columns(0, 0, HALF)
        store_codes(0)
        quantize_columns(1, 0, P)
        quantize_columns(1, P, HALF)
        store_codes(1)
        for q in range(4):
            queue = nc.sync if q % 2 == 0 else nc.scalar
            queue.dma_start(out_2[0, 4 * q : 4 * q + 4, :].bitcast(I32), out_scales[32 * q : 32 * q + 4, :].bitcast(I32))
